import numpy as np, ml_dtypes
CORES = [40,64,80,88,96,104,120,144]
N = 8
BF = ml_dtypes.bfloat16
def gentries(a):
    return np.ascontiguousarray(a.reshape(8, 16, -1).transpose(0, 2, 1)).reshape(8, -1)
def gtable(e):
    e = np.asarray(e); return np.ascontiguousarray(e.reshape(8, -1, 16).transpose(0, 2, 1)).reshape(128, -1).astype(np.int32)
NM, LN, T, S = 2048, 192, 3, 1
LIMS = (13, 10, 12)
WT = np.array([1, 16, 256, 37, 411, 93, 777, 165, 1029, 251, 1313, 339, 1583, 503, 1847, 618], np.int32)
KA = np.array([3, 61, 118, 207, 346, 419, 530, 677, 742, 895, 1011, 1164, 1283, 1450, 1629, 1874], np.int32)
LO = min(LIMS)
def parts(rng):
    lo = rng.choice(np.array([0.7, 0.85, 0.95], np.float32), (N, 8, 1, 1, 1)); h = lo + (1 - lo) * rng.random((N, 8, 1, 2, NM), dtype=np.float32)
    wr = np.minimum((16 * h * rng.random((N, 8, 16, 2, NM), dtype=np.float32)).astype(np.int32), 15)
    da = rng.integers(0, 16, (N, 8, 16, 2, NM), dtype=np.int32)
    ls = rng.integers(0, NM, (N, 8, LN, 16)); ls = np.where(rng.random((N, 8, LN, 1)) < 0.3, ls >> 3, ls)
    z = rng.integers(0, 16, (N, 8, 16, LN))
    ls[:, :, 1::8] = ls[:, :, 0::8]; z[..., 1::8] = z[..., 0::8]
    return wr, da, ls, z
def pack(wr, da, ls, z):
    return {"pg": np.ascontiguousarray((16 * wr + da).reshape(N, 128, 2 * NM)).astype(np.float32).astype(BF),
            "nm": np.stack([gtable(a.reshape(8, -1)) for a in ls]), "zv": np.ascontiguousarray(z.reshape(N, 128, LN)).astype(np.float32).astype(BF)}
def setup_inputs(rng):
    wr, da, ls, z = parts(rng)
    return pack(wr, da, ls, z)
def setup_inputs_spread(rng):
    wr, da, ls, z = parts(rng)
    p = np.exp2(rng.integers(-2, 3, (N, 8, 1, 2, NM))).astype(np.float32)
    wr = np.minimum((16 * rng.random((N, 8, 16, 2, NM), dtype=np.float32) ** p).astype(np.int32), 15)
    da = da & rng.choice(np.array([0, 1, 3, 8, 12, 15], np.int32), (N, 8, 16, 1, NM))
    ls = np.minimum((NM * rng.random((N, 8, LN, 16)) ** rng.choice(np.array([1.0, 2.0, 4.0]), (N, 8, LN, 1))).astype(np.int64), NM - 1)
    z = z & rng.choice(np.array([0, 1, 4, 7, 15, 15]), (N, 8, 16, LN))
    return pack(wr, da, ls, z)
def setup_inputs_ends(rng):
    kind = rng.choice(6, (N, 8, NM), p=np.array([0.12, 0.08, 0.06, 0.06, 0.38, 0.3])); k = kind[:, :, None, None, :]
    e = rng.integers(0, 2, (N, 8, 16, 2, NM), dtype=np.int16); both = rng.random((N, 8, 16, 1, NM), dtype=np.float32) < 0.4
    side = np.array([0, 1], np.int16).reshape(1, 1, 1, 2, 1)
    top = np.where(both, np.int16(1), e); top = np.where(k == 3, side, top); top = np.where(k == 2, 1 - side, top); top = np.where(k == 1, np.int16(1), top); top = np.where(k == 0, np.int16(0), top)
    under = np.where(rng.random((N, 8, 1, 1, NM)) < 0.5, LIMS[0] - 1, LO - 1).astype(np.int16)
    wr = np.where(k == 5, under, 15 * top).astype(np.int32); da = 15 * np.where(k == 5, e, top).astype(np.int32)
    u0 = int(15 * np.add.reduce(WT)) & (NM - 1); cm = ((u0 * u0 >> 5) + KA.astype(np.int64) * u0) & (NM - 1)
    for q in range(N):
        for g in range(8):
            if g in (2, 7): wr[q, g][:, :, cm] = LIMS[0] - 1
            a, b = (NM - 1, 0) if g in (1, 4) else (0, NM - 1)
            wr[q, g][:, :, a] = 0; da[q, g][:, :, a] = 0; wr[q, g][:, :, b] = 15; da[q, g][:, :, b] = 15
    wr[:, 6, :, :, 1:3] = 15; da[:, 6, :, :, 1:3] = 15
    pos = np.argsort(rng.random((N, 8, LN, 16)), axis=-1) < 10
    ls = np.where(pos, (NM - 1) * rng.integers(0, 2, pos.shape), rng.integers(0, NM, pos.shape))
    z = 15 * rng.integers(0, 2, (N, 8, 16, LN)); o = rng.integers(0, 8, (N, 8, 1, LN)); z = np.where(o == 0, 0, np.where(o == 1, 15, z))
    for q in range(N):
        some = np.setdiff1d(np.nonzero(kind[q, 7] == 5)[0], np.append(cm, [0, NM - 1]))
        ls[q, 7] = np.where(pos[q, 7], 0, rng.choice(some, (LN, 16)))
        ls[q, 7, LN - 1] = np.where(np.arange(16) % 2 == 1, NM - 1, 0)
        ls[q, 6, LN - 1, 0] = 2; ls[q, 6, LN - 1, 1] = 1; ls[q, 6, LN - 1, 2] = NM - 1
    z[:, 7, :, LN - 1] = 0; z[:, 6, :, LN - 1] = 0
    return pack(wr, da, ls, z)
def setup_inputs_corners(rng):
    wr, da, ls, z = parts(rng); rot = int(rng.integers(0, 8)); sh = (16, 2, NM)
    z[..., ::5] = 0; z[..., 2::5] = 15
    for q in range(N):
        for g in range(8):
            j = (g + q + rot) % 8; a = wr[q, g]; d = da[q, g]
            if j == 0:
                a[...] = rng.integers(0, LO, sh)
                n = np.append(np.sort(rng.permutation(NM - 1)[:3]), NM - 1); i = int(rng.integers(0, 16))
                d[:, :, n[:2]] = 15; d[i, :, n[0]] = 14; d[:, :, n[2:]] = 0; d[15 - i, :, n[2]] = 1
                ls[q, g, 0::10, 3] = n[0]; ls[q, g, 0::10, 15] = n[1]; ls[q, g, 2::10, 0] = n[3]; ls[q, g, 2::10, 9] = n[2]
            if j == 1:
                a[...] = 15; d[:, :, int(rng.integers(0, 64))::64] = 15
            if j == 2: a[...] = np.where(rng.random(sh) < 0.25, rng.choice(np.array([LO - 1, LO, LIMS[0] - 1, LIMS[0]]), sh), rng.integers(0, 4, sh))
            if j == 3:
                a[:, 0] = rng.integers(14, 16, (16, NM)); a[:, 1] = rng.integers(0, LO, (16, NM))
                d[:, :, ::2] = 0; z[q, g, :, ::2] = 0; ls[q, g, ::16] -= ls[q, g, ::16] & 1
            if j == 4: d[...] = rng.integers(0, 16, (16, 1, 1))
            if j == 5: a[:, 1] = a[:, 0]
            if j == 6:
                fresh = rng.permutation(NM)[:NM >> 4]; a[...] = 15; a[:, :, fresh] = rng.integers(0, LO, (16, 2, NM >> 4))
            if j == 7: ls[q, g] = rng.choice(np.array([0, 1, NM - 2, NM - 1]), (LN, 16))
    return pack(wr, da, ls, z)
def hang(rng, a, d, w, u):
    y = rng.integers(0, 16, (16, len(w))); y[:3] = 0
    v = (u - np.add.reduce(WT.astype(np.int64)[:, None] * y, axis=0)) & (NM - 1)
    y[0] = v & 15; y[1] = (v >> 4) & 15; y[2] = v >> 8
    a[:, :, w] = 15; d[:, :, w] = y[:, None, :]
def firsts():
    u = np.arange(NM, dtype=np.int64)
    return ((u * u >> 5)[:, None] + KA.astype(np.int64) * u[:, None]) & (NM - 1)
def mates(rng, a, w):
    v = np.add.reduce(a.reshape(32, NM), axis=0).astype(np.int64); v[w] = 1 << 20
    c = firsts()
    low = np.min(v[c] * NM + c, axis=1); b = np.where(low >= NM << 20, -1, low & (NM - 1))
    val, first = np.unique(b, return_index=True)
    return rng.permutation(first[val >= 0])
def setup_inputs_crowd(rng):
    wr, da, ls, z = parts(rng); pr = rng.permutation(N)
    for q in range(N):
        for g in range(8):
            a = wr[q, g]; d = da[q, g]; a[...] = rng.integers(0, 3, (16, 2, NM)); j = (g + q) % 8
            o = rng.permutation(NM)
            if j == 6: o = o[o > 0]
            w = o[:LN]
            if q == pr[0] or q == pr[1]:
                old = o[LN:LN + (NM >> 3)]; a[:, :, old] = 15; d[:, :, old] = 15 * rng.integers(0, 2, (16, 1, len(old)))
                hang(rng, a, d, w, np.resize(mates(rng, a, np.append(w, old)), LN)); ls[q, g] = w[:, None]
                if q == pr[1] and g == 7: ls[q, g, LN - 1] = w[0]
            elif j < 2:
                us = np.resize(mates(rng, a, w), LN); hang(rng, a, d, w[:2], us[:2]); ls[q, g] = w[0]
                if j == 1: ls[q, g, LN - 1] = w[1]
            elif j < 4:
                us = np.resize(mates(rng, a, w), LN); one = np.full(LN, us[0])
                if j == 3: one[LN - 1] = us[1]
                hang(rng, a, d, w, one); ls[q, g] = w[:, None]
            elif j < 6:
                ls[q, g] = w[:, None]
                if j == 5: ls[q, g, LN - 1] = w[0]
            elif j == 6:
                a[:, :, 0] = 0; us = np.nonzero(np.any(firsts() == 0, axis=1))[0]
                hang(rng, a, d, w, np.full(LN, int(rng.choice(us)))); ls[q, g] = w[:, None]
            else:
                a[...] = rng.integers(LIMS[0] - 2, LIMS[0], (16, 2, NM)); sp = o[LN:LN + (NM >> 2)]; a[:, :, sp] = 0
                a[rng.integers(0, 16, len(sp)), rng.integers(0, 2, len(sp)), sp] = 15
                hang(rng, a, d, w, rng.permutation(NM)[:LN]); ls[q, g] = w[:, None]
    return pack(wr, da, ls, z)
def check_inputs(d):
    bad = []
    for k, hi in (("pg", 255), ("nm", NM - 1), ("zv", 15)):
        x = np.asarray(d[k]).astype(np.float32)
        if not np.all((x >= 0) & (x <= hi) & (x == np.floor(x))): bad.append("range of " + k)
    return bad
def pick(a, ix):
    return np.take_along_axis(a, ix[:, :, None, :], 3)
def reference(pg, nm, zv):
    v = pg.astype(np.float32).astype(np.int32).reshape(N, 8, 16, 2, NM); wr = v >> 4; da = v & 15
    ls = np.stack([gentries(a) for a in nm]).astype(np.int32)
    z = zv.astype(np.float32).astype(np.int32).reshape(N, 8, 16, LN)
    A = np.zeros((N, 1, 1, 1), np.int32); low = np.tril(np.ones((LN, LN), bool), -1); NONE = 1 << 30
    for t in range(T):
        lim = LIMS[t]
        if t > 0: ls = np.roll(ls, S, axis=0); z = np.roll(z, S, axis=0)
        f = wr[:, :, :, 0]; s = wr[:, :, :, 1]
        y = np.where(f <= s, da[:, :, :, 0], da[:, :, :, 1])
        lk = ls.reshape(N, 8, LN, 16)
        sc = np.add.reduce(np.abs(pick(y, ls).reshape(N, 8, 16, LN, 16) - z[..., None]), axis=2).astype(np.int32)
        w = NM - 1 - (np.max(sc * NM + (NM - 1 - lk), axis=3) & (NM - 1))
        yw = pick(y, w); fw = pick(f, w); sw = pick(s, w)
        u = (np.add.reduce(WT[:, None] * yw, axis=2) & (NM - 1)).astype(np.int32)
        faulty = np.any((fw >= lim) & (sw >= lim), axis=2)
        c = ((u * u >> 5)[..., None] + KA * u[..., None] + A) & (NM - 1)
        cx = c.reshape(N, 8, LN * 16)
        m1 = np.minimum(fw[..., None], pick(s, cx).reshape(N, 8, 16, LN, 16)); m2 = np.minimum(pick(f, cx).reshape(N, 8, 16, LN, 16), sw[..., None])
        ok = np.max(np.maximum(m1, m2), axis=2) < lim
        best = np.min(np.where(ok, np.add.reduce(m1 + m2, axis=2) * NM + c, NONE), axis=3)
        has = faulty & (best < NONE); cl = np.where(has, best & (NM - 1), -1)
        wa, wb, ca, cb = w[:, :, :, None], w[:, :, None, :], cl[:, :, :, None], cl[:, :, None, :]
        hit = (wa == wb) | (wa == cb) | (ca == wb) | ((ca == cb) & (ca >= 0))
        com = ~np.any(hit & low, axis=3)
        q, g, l = np.nonzero(com & ~faulty); n = w[q, g, l]
        zn = z[q, g, :, l][:, :, None]; od = da[q, g, :, :, n]; ow = wr[q, g, :, :, n]
        nw = np.minimum(15, ow + (od != zn))
        ex = com & has; q2, g2, l2 = np.nonzero(ex); n2 = w[q2, g2, l2]; o2 = cl[q2, g2, l2]
        a1 = wr[q2, g2, :, 1, n2]; b1 = wr[q2, g2, :, 1, o2]; ya = y[q2, g2, :, n2]; yb = y[q2, g2, :, o2]
        wr[q, g, :, :, n] = nw; da[q, g, :, :, n] = zn
        wr[q2, g2, :, 1, n2] = b1; wr[q2, g2, :, 1, o2] = a1
        da[q2, g2, :, :, n2] = ya[:, :, None]; da[q2, g2, :, :, o2] = yb[:, :, None]
        A = np.add.reduce(ex.reshape(N, -1).astype(np.int32), axis=1).astype(np.int32).reshape(N, 1, 1, 1)
        k = np.arange(16 * LN, dtype=np.int32).reshape(LN, 16)
        ls = (((lk * (2 * (u & 1023) + 1)[..., None] >> 5) + lk + 37 * k) & (NM - 1)).reshape(N, 8, 16 * LN)
        z = np.abs(z - yw)
    e = 16 * wr + da
    return {"ys": np.ascontiguousarray(e[:, :, :, 1].reshape(N, 128, NM)).astype(np.float32).astype(BF),
            "yf": np.add.reduce(e[:, :, :, 0].reshape(N, 128, NM >> 6, 64), axis=2).astype(np.float32),
            "yn": np.stack([gtable(a) for a in ls]).astype(np.float32),
            "yz": np.ascontiguousarray(z.reshape(N, 128, LN)).astype(np.float32).astype(BF)}

@@ -1,0 +1,800 @@
+from concourse.bass import DstId, RemoteDMATransfer
+from concourse.mybir import AluOpType as OP, AxisListType as AX, ActivationFunctionType as AF
+
+NM, LN = 2048, 192
+LIMS = (13, 10, 12)
+WT = (1, 16, 256, 37, 411, 93, 777, 165, 1029, 251, 1313, 339, 1583, 503, 1847, 618)
+KA = (3, 61, 118, 207, 346, 419, 530, 677, 742, 895, 1011, 1164, 1283, 1450, 1629, 1874)
+GS = 2432
+BIG = 2048000.0
+RND = 128.53125
+
+SCRATCH = {}
+
+
+def _decl(dtype, spec, where="sbuf"):
+    for item in spec.split():
+        name, n = item.split(":")
+        SCRATCH[name] = (where, [128, int(n)], dtype)
+
+
+_decl("bfloat16", "P2:2432 Y:4672 W:4096 G0:4864 G1:4864 G2:4864 ZY0:384 ZY1:384 ZY2:384 SZ0:192 SZ1:192 SZ2:192 "
+      "ga:3072 gb:3072 ma:3072 mb:3072 E:9216 I1:128 Im1:128 I16:128 Im16:128 Bp4:144 Bm4:144 Bp2:144 BO:128 BOh:128 "
+      "BOl:128 GW:384 M17:192 PW:384 WX:576 SG:384 NE:384 RR:384 JJ:384 SP:384 VV:192 VP1:384 VP2:384 VG:384 VD:384 "
+      "XC:384 WC:192 YC:192")
+_decl("float16", "L16:384")
+_decl("float32", "LC:2240 IF:128 ONE:128 X:144 X2:128 col:16 JX:12 t24:24 u24:24 t12:12 REPf:12 KT:192 K32:192 DM:192 DR:192 "
+      "TH:384 KH:384 ZH:384 UP:192 UQ:192 HF:192 ZR:192 WL:192 KP:192 DG:192 DT:64 TT:64 OA:64 OB:64 OF:64 L:192 D384:384 T384:384 ZS:192 "
+      "USQ:12 KU:192 CT:192 FB:12 VF:16 S7:192 nar:128 YF:64 WTT:32 TR:112 TS:72 TU:72")
+_decl("int32", "NI:192 IP:8 WI:24 U0:24 UI:16 BS:16 C0:192 CI:192 S8:192 S9:192 CE:24")
+_decl("uint16", "NU0:192 NU1:192 NU2:192 SN0:192 SN1:192 REP:12 R16:4 PERM:12 DUP:24 INV1:24 INV2:12 WU:36 CU:192 "
+      "CEU:12 SEL:12 OU0:64 OU1:64")
+_decl("float32", "pz:512 pk:512 pu:512 pa:512 pb:512 ph:512 px:512 py:512", "psum")
+
+NDMA = 28
+SEMAPHORES = ["cP", "cV", "cS", "cG", "arr1", "arr2", "left1", "left2"] + ["d%d" % i for i in range(NDMA)]
+PAR = {"cy": 1.0, "g": 1.5, "sc": 3.5, "pe": 0.42, "wake": 70.0, "bw": 180.0, "hop": 8000.0, "rounds": 40,
+       "moves": 800, "mix": 0.0, "noise": 600.0, "seed": 4, "ca": (1, 2, 3, 1, 1), "cb": (1, 2, 2, 2, 1), "piece": 12, "na": 1,
+       "q0": "VVVVVVVV", "q1": "SSSSSSSS", "q2": "VVVVSSSS", "qw": "VVVV", "s2": 1, "cc": ((0, 192),), "nd": 4}
+ORDER = {}
+PART = {"P1": ("Y", 2240, GS), "J0": ("mb", -1024, 4096), "WU": ("WU", 0, 12), "WCU": ("WU", 12, 24),
+        "WH": ("IP", 4, 4), "K0": ("WI", 12, 12), "V0": ("U0", 12, 12), "E0": ("CE", 12, 12),
+        "WI": ("WI", 0, 12), "U0": ("U0", 0, 12), "CE": ("CE", 0, 12), "EX": ("nar", 112, 16), "AC": ("col", 12, 1)}
+
+
+def A(name, c0=0, c1=None, step=1):
+    if name in PART:
+        name, at, n = PART[name]
+        return (name, at + c0, at + (n if c1 is None else c1), step)
+    if c1 is None:
+        c1 = SCRATCH[name][1][1]
+    return (name, c0, c1, step)
+
+
+def _overlap(a, b):
+    if a[1] >= b[2] or b[1] >= a[2]:
+        return False
+    if a[3] == b[3] and a[3] > 1:
+        return (a[1] - b[1]) % a[3] == 0
+    return True
+
+
+def _relay(src, dst, T, topo):
+    if topo.may_write(src, dst):
+        return None
+    free = [c for c in topo.cores_of(src) if c != src and T.rank_of(c) is None and topo.may_write(c, dst)]
+    near = [c for c in free if topo.die(c) == topo.die(src)]
+    return (near or free)[0]
+
+
+def _send(g, T, topo, src, dst, t, names, vec):
+    eng = topo.engines(src, dst)
+    half = len(eng) // 2
+    rid, pid = topo.addr(dst, src)
+    sem = T.sem["arr%d" % t]
+    trs = []
+    for part, s, d in ((eng[:half], names, T["NU%d" % t][:, 0:LN]), (eng[half:2 * half], vec, T["ZY%d" % t][:, 0:LN])):
+        trs.append(RemoteDMATransfer(dst_ids=[DstId(rid=rid, pnc=pid)], dma_engine_mask=sum(1 << e for e in part),
+                                     remote_sem=sem, src=s, dst=d))
+    g.remote_dma_fused(trs, local_sem=T.sem["left%d" % t])
+    return 2 * half
+
+
+def _count(src, dst, topo):
+    return 2 * (len(topo.engines(src, dst)) // 2)
+
+
+def rank_program(g, core, T, topo):
+    cores = list(T.cores)
+    n = len(cores)
+    rank = T.rank_of(core)
+    if rank is None:
+        for r in range(n):
+            dst = cores[(r + 1) % n]
+            if _relay(cores[r], dst, T, topo) == core:
+                for t in (1, 2):
+                    g.wait_ge(T.sem["arr%d" % t], _count(cores[r], core, topo))
+                    k = _send(g, T, topo, core, dst, t, T["NU%d" % t][:, 0:LN], T["ZY%d" % t][:, 0:LN])
+                for t in (1, 2):
+                    g.wait_ge(T.sem["left%d" % t], k)
+        return
+    nxt, prv = cores[(rank + 1) % n], cores[(rank - 1) % n]
+    hop = _relay(core, nxt, T, topo)
+    hop = nxt if hop is None else hop
+    frm = _relay(prv, core, T, topo)
+    frm = prv if frm is None else frm
+    ops = []
+    build(ops, T, g, lambda t: _send(g, T, topo, core, hop, t, T["SN%d" % (t - 1)][:, 0:LN], T["SZ%d" % (t - 1)][:, 0:LN]))
+    if "order" not in ORDER:
+        ORDER["deps"], soft = hazards(ops)
+        ORDER["order"] = schedule(ops, ORDER["deps"], soft)
+    emit(ops, ORDER["deps"], ORDER["order"], T, g, _count(frm, core, topo), _count(core, hop, topo))
+
+
+def hazards(ops):
+    hist, deps, soft, sends = {}, [], [], {}
+    for k, o in enumerate(ops):
+        d, s = set(), set()
+        accs = [(a, False) for a in o["r"]] + [(a, True) for a in o["w"]]
+        for acc, wr in accs:
+            psum = SCRATCH[acc[0]][0] == "psum"
+            for j, b, bw in hist.get(acc[0], ()):
+                same = ops[j]["q"] == o["q"] and ops[j]["kind"] == "c" and o["kind"] == "c"
+                if same and o["q"] == "P":
+                    if psum:
+                        s.add(j)
+                elif (psum and not same) or ((wr or bw) and _overlap(acc, b)):
+                    d.add(j)
+        for acc, wr in accs:
+            h = hist.setdefault(acc[0], [])
+            if SCRATCH[acc[0]][0] == "psum":
+                if o["q"] == "P":
+                    h[:] = []
+            elif wr and acc[3] == 1:
+                h[:] = [e for e in h if not (acc[1] <= e[1][1] and e[1][2] <= acc[2])]
+            h.append((k, acc, wr))
+        s.update(o.get("after", ()))
+        if o["kind"] == "send":
+            sends[o["t"]] = k
+        if o["kind"] == "arr":
+            s.add(sends[o["t"]])
+        deps.append(d)
+        soft.append(s)
+    return deps, soft
+
+
+def schedule(ops, deps, soft):
+    n = len(ops)
+    cost = [o["cost"] for o in ops]
+    fwd = [[] for _ in range(n)]
+    bwd = [[] for _ in range(n)]
+    for k in range(n):
+        for j in sorted(deps[k] | soft[k]):
+            if j in deps[k]:
+                gap = cost[j] + ops[j]["lat"] + PAR["wake"]
+            else:
+                gap = cost[j] + (PAR["hop"] if ops[k]["kind"] == "arr" else 0.0)
+            fwd[j].append((k, gap))
+            bwd[k].append((j, gap + cost[k] - cost[j]))
+
+    def place(succ, pred, ready, prio, wires):
+        left = [len(p) for p in pred]
+        cand = [k for k in range(n) if left[k] == 0]
+        busy = {q: [] for q in "PVSGY"}
+        start, end = [0.0] * n, 0.0
+        wire = []
+        while cand:
+            c = max(cand, key=lambda k: (prio[k], -k))
+            cand.remove(c)
+            line, t = busy[ops[c]["q"]], ready[c]
+            lo, hi = 0, len(line)
+            while lo < hi:
+                mid = (lo + hi) // 2
+                if line[mid][1] <= t:
+                    lo = mid + 1
+                else:
+                    hi = mid
+            while lo < len(line) and line[lo][0] < t + cost[c]:
+                t = max(t, line[lo][1])
+                lo += 1
+            line.insert(lo, (t, t + cost[c]))
+            start[c] = t
+            extra = 0.0
+            if wires and ops[c]["kind"] in ("d", "send"):
+                w0, d = t + cost[c] + 1500.0, max(ops[c]["lat"] - 1500.0, 600.0)
+                w = max([w0] + [y for x, y in wire if x <= t])
+                wire.append((t, w + d))
+                extra = w - w0
+            end = max(end, t + cost[c] + ops[c]["lat"] + extra)
+            for k, gap in succ[c]:
+                ready[k] = max(ready[k], t + gap + (extra if gap > cost[c] + 1 else 0.0))
+                left[k] -= 1
+                if left[k] == 0:
+                    cand.append(k)
+        return start, end
+
+    prio = [0.0] * n
+    for j in reversed(range(n)):
+        prio[j] = max([cost[j] + ops[j]["lat"]] + [gap + prio[k] for k, gap in fwd[j]])
+    best, seed = None, PAR["seed"]
+    for r in range(PAR["rounds"]):
+        for k in range(n):
+            if ops[k]["kind"] == "d" and not ops[k]["r"]:
+                prio[k] = 1e9 - k
+        st, end = place(fwd, bwd, [0.0] * n, prio, True)
+        if best is None or end < best[0]:
+            best = (end, st)
+        if r % 2:
+            st = best[1]
+        back = place(bwd, fwd, [o["lat"] for o in ops], [st[k] + cost[k] for k in range(n)], False)[0]
+        prio = []
+        for k in range(n):
+            seed = (seed * 1103515245 + 12345) % 2147483648
+            mix = PAR["mix"] * (best[0] - best[1][k]) + (1 - PAR["mix"]) * (back[k] + cost[k])
+            prio.append(mix + PAR["noise"] * seed / 2147483648.0)
+    for r in range(PAR["moves"]):
+        st = best[1]
+        if r == 0 or fresh:
+            prev, last = {}, {}
+            for k in sorted(range(n), key=lambda k: st[k]):
+                prev[k] = last.get(ops[k]["q"])
+                last[ops[k]["q"]] = k
+            k, held = max(range(n), key=lambda k: st[k] + cost[k] + ops[k]["lat"]), []
+            while k is not None:
+                j = prev[k]
+                if j is not None and st[j] + cost[j] >= st[k] - 1 and j not in soft[k]:
+                    held.append((j, k))
+                    k = j
+                else:
+                    k = max((j for j, gap in bwd[k]), key=lambda j: st[j] + cost[j] + ops[j]["lat"], default=None)
+        seed = (seed * 1103515245 + 12345) % 2147483648
+        j, k = held[(seed >> 8) % len(held)]
+        seed = (seed * 1103515245 + 12345) % 2147483648
+        prio = [-s for s in st]
+        step = 100.0 * 1.5 ** ((seed >> 8) % 12)
+        if (seed >> 20) % 3 == 2:
+            prio[j] -= step + cost[k]
+        else:
+            todo = [k if (seed >> 20) % 3 == 0 else j]
+            prio[todo[0]] = prio[j] + step
+            while todo:
+                c = todo.pop()
+                for a, gap in bwd[c]:
+                    want = prio[c] + gap + cost[a] - cost[c]
+                    if prio[a] < want - 1:
+                        prio[a] = want
+                        todo.append(a)
+        new, end = place(fwd, bwd, [0.0] * n, prio, True)
+        fresh = end <= best[0]
+        if fresh:
+            best = (end, new)
+    ORDER["end"] = best[0]
+    return sorted(range(n), key=lambda k: (best[1][k], k))
+
+
+def emit(ops, deps, order, T, g, n_arr, n_left):
+    queue = {"P": g.tensor, "V": g.vector, "S": g.scalar, "G": g, "Y": g.sync}
+    pos = {k: i for i, k in enumerate(order)}
+    seen = {q: {} for q in queue}
+    need, keep = set(), {}
+    for k in order:
+        o = ops[k]
+        last_p = max([pos[j] for j in deps[k] if ops[j]["q"] == "P"], default=-1)
+        kd = [j for j in deps[k] if (ops[j]["q"] != "P" or pos[j] == last_p) and
+              not (ops[j]["kind"] == "c" and seen[o["q"]].get(ops[j]["q"], -1) >= pos[j])]
+        need.update(kd)
+        for j in kd:
+            if ops[j]["kind"] == "c":
+                seen[o["q"]][ops[j]["q"]] = max(seen[o["q"]].get(ops[j]["q"], -1), pos[j])
+        keep[k] = kd
+    cnt = {q: 0 for q in "PVSG"}
+    mark, total, ndma = {}, {}, 0
+    waited = {q: {} for q in queue}
+    for k in order:
+        o = ops[k]
+        want = {}
+        for j in keep[k]:
+            s, v = mark[j]
+            want[s] = max(want.get(s, 0), v)
+        for s, v in sorted(want.items()):
+            if waited[o["q"]].get(s, 0) < v:
+                queue[o["q"]].wait_ge(T.sem[s], v)
+                waited[o["q"]][s] = v
+        if o["kind"] == "arr":
+            mark[k] = ("arr%d" % o["t"], n_arr)
+            total[mark[k][0]] = n_arr
+            continue
+        ins = o["f"]()
+        if o["kind"] == "send":
+            total["left%d" % o["t"]] = n_left
+        elif o["kind"] == "d":
+            s = "d%d" % ndma
+            ndma += 1
+            ins.then_inc(T.sem[s], 16)
+            mark[k] = (s, 16)
+            total[s] = 16
+        elif k in need:
+            cnt[o["q"]] += 1
+            ins.then_inc(T.sem["c" + o["q"]], 1)
+            mark[k] = ("c" + o["q"], cnt[o["q"]])
+            total["c" + o["q"]] = cnt[o["q"]]
+    for s, v in sorted(total.items()):
+        if max(w.get(s, 0) for w in waited.values()) < v:
+            g.wait_ge(T.sem[s], v)
+
+
+def build(ops, T, g, send):
+    V, S, PE = g.vector, g.scalar, g.tensor
+    size = {"bfloat16": 2, "float16": 2, "uint16": 2, "float32": 4, "int32": 4}
+
+    def ap(a):
+        if a[0] == "ind":
+            return ap(a[1]).indirect(ap(a[2]))
+        if a[3] == 1:
+            return T[a[0]][:, a[1]:a[2]]
+        return T[a[0]][:, a[1]:a[2]:a[3]]
+
+    def width(a):
+        return 16 * width(a[2]) if a[0] == "ind" else len(range(a[1], a[2], a[3]))
+
+    def add(q, f, w, r, k=1.0, kind="c", t=0, cost=None, lat=0.0):
+        rs = []
+        for a in r:
+            if isinstance(a, tuple):
+                rs += [a[1], a[2]] if a[0] == "ind" else [a]
+        if cost is None:
+            if w[0] == "ind":
+                cost = 50 + width(w) * PAR["sc"] * PAR["cy"]
+            elif r and r[0][0] == "ind":
+                cost = 50 + width(w) * PAR["g"] * PAR["cy"]
+            else:
+                cost = max(64, width(r[0] if r else w) * k) * PAR["cy"]
+            cost += 15 if q == "S" else 0
+        if w is not None and w[0] == "ind":
+            rs.append(w[2])
+            w = w[1]
+        ops.append({"q": q, "f": f, "w": [] if w is None else [w], "r": rs, "kind": kind, "t": t, "cost": cost, "lat": lat})
+        if spine["on"] and q in "VS" and kind == "c":
+            ops[-1]["after"] = [spine[q]] if q in spine else []
+            spine[q] = len(ops) - 1
+
+    spine = {"on": False}
+
+    def fixed(on):
+        spine["on"] = on
+
+    def val(x):
+        return ap(x) if isinstance(x, tuple) else x
+
+    def ind(win, off):
+        return ("ind", win, off)
+
+    def two(o, a):
+        return 0.5 if "ind" not in (o[0], a[0]) and size[SCRATCH[o[0]][2]] == 2 and size[SCRATCH[a[0]][2]] == 2 else 1.0
+
+    def cp(o, i):
+        add("V", lambda: V.tensor_copy(ap(o), ap(i)), o, [i], two(o, i))
+
+    def tt(o, a, b, op):
+        k = 1.0 if a[0] == "ind" or "psum" in (SCRATCH[a[0]][0], SCRATCH[b[0]][0]) else 2.0
+        add("V", lambda: V.tensor_tensor(ap(o), ap(a), ap(b), op), o, [a, b], k)
+
+    def ts(o, a, s1, op0, s2=None, op1=None):
+        if op1 is None:
+            add("V", lambda: V.tensor_scalar(ap(o), ap(a), val(s1), None, op0), o, [a, s1], two(o, a))
+        else:
+            add("V", lambda: V.tensor_scalar(ap(o), ap(a), val(s1), val(s2), op0, op1), o, [a, s1, s2], two(o, a))
+
+    def red(o, a, op):
+        add("V", lambda: V.tensor_reduce(ap(o), ap(a), AX.X, op), o, [a])
+
+    def scan(o, a, b, init, op0, op1):
+        add("V", lambda: V.tensor_tensor_scan(ap(o), ap(a), ap(b), init, op0, op1), o, [a, b])
+
+    def tr(o, a):
+        add("V", lambda: V.transpose(ap(o), ap(a)), o, [a])
+
+    def ms(o, c):
+        add("V", lambda: V.memset(ap(o), c), o, [])
+
+    def act(o, a, func=AF.Identity, bias=0.0, scale=1.0):
+        add("S", lambda: S.activation(ap(o), ap(a), func, bias=bias, scale=scale), o, [a])
+
+    def mm(o, l, r, start, stop):
+        add("P", lambda: PE.matmul(ap(o), ap(l), ap(r), start, stop), o, [l, r],
+            cost=max(64, width(r)) * PAR["pe"] * (4 if size[SCRATCH[l[0]][2]] == 4 else 1), lat=100.0)
+
+    def lin(o, terms):
+        for k, (l, r) in enumerate(terms):
+            mm(o, A(l), r, k == 0, k == len(terms) - 1)
+
+    def iota(o, pat, base=0, ch=0):
+        cost = 130 + 2 * width(o) * PAR["cy"]
+        if SCRATCH[o[0]][2] == "int32":
+            add("G", lambda: g.iota(ap(o), pat, base, ch), o, [], cost=cost)
+        else:
+            add("G", lambda: g.iota(ap(o), pat, base, ch, allow_small_or_imprecise_dtypes=True), o, [], cost=cost)
+
+    def fill(o, c=0):
+        iota(o, [[0, width(o)]], c)
+
+    def wire(a, k=1):
+        return 1500.0 + k * 128 * width(a) * size[SCRATCH[a[0]][2]] / PAR["bw"]
+
+    def load(q, o, src):
+        add(q, lambda: {"Y": g.sync, "S": g.scalar}[q].dma_start(ap(o), src), o, [], kind="d", cost=100.0, lat=wire(o))
+
+    def store(q, dst, i):
+        add(q, lambda: {"Y": g.sync, "S": g.scalar}[q].dma_start(dst, ap(i)), None, [i], kind="d", cost=100.0, lat=wire(i))
+
+    def dadd(o, i):
+        add("G", lambda: g.dma_start(ap(o), ap(i), accum_op=OP.add), o, [i, o], kind="d", cost=500.0, lat=wire(o, 2))
+
+    pf, rf, p31, g16, g15, c16, r12, r16, whi, wlo, wt = [A("col", k, k + 1) for k in range(11)]
+    lane = A("JX")
+
+    load("Y", A("NI"), T.nm[:, :])
+    for k in range(4):
+        load("S", A("P2", 512 * k, 512 * k + 512), T.pg[:, NM + 512 * k:NM + 512 * k + 512])
+        load("Y", A("P1", 512 * k, 512 * k + 512), T.pg[:, 512 * k:512 * k + 512])
+    load("S", A("ZY0", 0, LN), T.zv[:, :])
+    for k in range(1, len(ops)):
+        ops[k]["after"] = [k - 1]
+    due = {}
+
+    def before(tag):
+        due.setdefault(tag, []).append(len(ops) - 1)
+
+    def behind(tag):
+        ops[-1]["after"] = ops[-1].get("after", []) + due.pop(tag, [])
+
+    iota(A("IP", 0, 1), [[0, 1]], 0, 1)
+    iota(A("FB"), [[16, 12]])
+    iota(A("t24"), [[16, 12], [0, 2]])
+    iota(A("u24"), [[1, 12], [0, 2]])
+    iota(A("X"), [[1, 144]])
+    iota(A("X2"), [[16, 8], [0, 16]])
+    iota(A("DR"), [[0, 12], [1, 16]])
+    iota(A("K32"), [[1, 16], [256, 12]])
+    iota(A("LC"), [[1, 2240]], -1024)
+    for m in range(16):
+        iota(A("WTT", m, m + 1), [[0, 1]], WT[m])
+        iota(A("KT", 12 * m, 12 * m + 12), [[0, 12]], KA[m])
+    for a in (A("P1", NM, GS), A("P2", NM, GS), A("ZR"), A("DT", 60, 64), A("TT", 60, 64)):
+        fill(a)
+    for name in ("G1", "G2"):
+        fill(A(name, NM, GS))
+        fill(A(name, GS + NM, 2 * GS))
+    fill(A("ONE"), 1)
+    cp(pf, A("IP", 0, 1))
+    ts(A("IP", 1, 2), A("IP", 0, 1), 15, OP.bitwise_and)
+    ts(A("IP", 2, 3), A("IP", 0, 1), 31, OP.bitwise_and)
+    cp(rf, A("IP", 1, 2))
+    cp(p31, A("IP", 2, 3))
+    ts(A("INV2"), A("FB"), 2.0, OP.mult, p31, OP.add)
+    ts(A("DUP"), A("t24"), rf, OP.add)
+    ts(lane, A("FB"), rf, OP.add)
+    tt(c16, p31, rf, OP.subtract)
+    tt(g16, pf, rf, OP.subtract)
+    ts(A("K0"), lane, 1.0 / 12, OP.mult, -0.458, OP.add)
+    for name, c in (("I1", 1.0), ("Im1", -1.0), ("Im16", -16.0), ("I16", 16.0), ("IF", 1.0)):
+        ts(A(name), A("X", 0, 128), pf, OP.is_equal, c, OP.mult)
+    ts(A("t12"), A("K0"), -12.0, OP.mult)
+    ts(g15, g16, 15.0, OP.add)
+    tt(A("REPf"), A("t12"), lane, OP.add)
+    ts(A("t12"), A("REPf"), 32.0, OP.mult, c16, OP.add)
+    tt(A("t12"), A("t12"), A("K0"), OP.add)
+    cp(A("PERM"), A("t12"))
+    cp(A("REP"), A("REPf"))
+    for name, c in (("Bp2", 2048.0), ("Bm4", -4096.0), ("Bp4", 4096.0)):
+        ts(A(name), A("X"), g15, OP.is_equal, c, OP.mult)
+    ts(A("KP"), A("DR"), 0.0, OP.not_equal)
+    ts(A("DM"), A("DR"), rf, OP.is_equal)
+    ts(A("DG"), A("DR"), rf, OP.is_equal, 262144.0, OP.mult)
+    ts(A("BO"), A("X2"), g16, OP.is_equal)
+    tt(A("WTT", 16, 32), A("WTT", 0, 16), A("DM", 0, 16), OP.mult)
+    red(wt, A("WTT", 16, 32), OP.add)
+    cp(A("WH", 0, 1), wt)
+    ts(A("WH", 1, 2), A("WH", 0, 1), 15, OP.bitwise_and)
+    cp(wlo, A("WH", 1, 2))
+    tt(whi, wt, wlo, OP.subtract)
+    ts(A("BOl"), A("X2"), g16, OP.is_equal, wlo, OP.mult)
+    ts(A("BOh"), A("X2"), g16, OP.is_equal, whi, OP.mult)
+    ms(A("AC"), -0.484375)
+    ts(r16, rf, 16.0, OP.mult)
+    ts(A("K32"), A("K32"), r16, OP.add, 1184.0, OP.mult)
+    ms(A("HF"), 0.5)
+    scan(A("UP"), A("HF"), A("ZR"), 2.0 ** 96, OP.mult, OP.add)
+    tt(A("UQ"), A("UP"), A("DM"), OP.mult)
+    scan(A("WL"), A("KP"), A("UQ"), 0.0, OP.mult, OP.max)
+    iota(A("KH"), [[0, 12], [1, 32]])
+    iota(A("TH"), [[0, 24], [1, 16]])
+    ts(A("KH"), A("KH"), 0.0, OP.not_equal)
+    ts(A("TH"), A("TH"), rf, OP.not_equal, -2.0 ** 99, OP.mult)
+    ts(A("ZH"), ind(A("UQ"), A("DUP")), -2.5, OP.mult)
+    for k, c in enumerate((2240 + 2048.0, 2240.0, 2048.0, GS + 2240.0, GS + 2048.0)):
+        ts(A("DT", 12 * k, 12 * k + 12), lane, c, OP.add)
+    ts(A("R16"), A("REPf", 0, 4), 32.0, OP.mult, 31.0, OP.add)
+    ts(r12, rf, 12.0, OP.mult)
+    ts(A("INV1"), A("u24"), r12, OP.add)
+    cp(A("D384"), ind(A("NI"), A("DUP")))
+    tr(A("T384"), A("D384"))
+    cp(A("L"), ind(A("T384"), A("PERM")))
+    cp(A("NU0"), A("L"))
+
+    for k in range(8):
+        c0, c1 = 256 * k, 256 * k + 256
+        b = (("pa", "pb"), ("ph", "px"), ("py", "pu"))[k % 3]
+        sel, dif, wm = A("ga", c0, c1), A("gb", c0, c1), A("ma", c0, c1)
+        ts(A("W", NM + c0, NM + c1), A("P2", c0, c1), 1.0 / 16, OP.mult, RND, OP.add)
+        if PAR["qw"][k // 2] == "V":
+            ts(A("W", c0, c1), A("P1", c0, c1), 1.0 / 16, OP.mult, RND, OP.add)
+        else:
+            act(A("W", c0, c1), A("P1", c0, c1), bias=RND, scale=1.0 / 16)
+        lin(A(b[0], 256, 512), [("I1", A("P1", c0, c1)), ("Im1", A("P2", c0, c1))])
+        lin(A(b[0], 0, 256), [("I1", A("W", c0, c1))])
+        tt(sel, A(b[0], 0, 256), A("W", NM + c0, NM + c1), OP.is_le)
+        tt(dif, A(b[0], 256, 512), sel, OP.mult)
+        mm(A(b[1], 0, 256), A("I1"), A("P2", c0, c1), True, False)
+        mm(A(b[1], 0, 256), A("I1"), dif, False, True)
+        act(wm, A(b[1], 0, 256), bias=RND, scale=1.0 / 16)
+        lin(A(b[0], 0, 256), [("I1", A("P2", c0, c1)), ("I1", dif), ("Im16", wm)])
+        act(A("Y", c0, c1), A(b[0], 0, 256), bias=2064.0)
+
+    def over(q, o, t, c0, c1):
+        if q == "V":
+            ts(o, A("W", c0, c1), 129.0 + LIMS[t], OP.is_ge, 1024.0, OP.mult)
+        else:
+            act(o, A("W", c0, c1), AF.Relu, bias=-1024.0 * (128 + LIMS[t]), scale=1024.0)
+
+    def table(t, qs):
+        for h in (0, 1):
+            for k in range(4):
+                over(qs[4 * h + k], A("G%d" % t, GS * h + 512 * k, GS * h + 512 * k + 512), t, NM * h + 512 * k, NM * h + 512 * k + 512)
+            dadd(A("G%d" % t, GS * h, GS * h + NM), A("W", NM * h, NM * h + NM))
+            behind("add")
+            before("add")
+
+    def table0():
+        nd = PAR["nd"]
+        for k in range(nd):
+            c0, o0 = 512 * k, GS * (k // 4) + 512 * (k % 4)
+            over(PAR["q0"][k], A("G0", o0, o0 + 512), 0, c0, c0 + 512)
+            if k % 2:
+                dadd(A("G0", o0 - 512, o0 + 512), A("W", c0 - 512, c0 + 512))
+                before("add")
+        for k in range(nd, 8):
+            c0, c1 = 512 * k, 512 * k + 512
+            b = A(("ph", "px", "py")[k % 3])
+            over(PAR["q0"][k], A("J0", c0, c1), 0, c0, c1)
+            lin(b, [("I1", A("W", c0, c1)), ("I1", A("J0", c0, c1))])
+            o = A("G0", GS * (k // 4) + c0 % NM, GS * (k // 4) + c0 % NM + 512)
+            if k in PAR.get("v0", ()):
+                cp(o, b)
+            else:
+                act(o, b, AF.Copy)
+
+    S2, S4 = ((0, 72), (72, 144), (144, 192)), ((0, 96), (96, 168), (168, 192))
+
+    def least2(banks, out):
+        act(A("TR", 0, 72), A(banks[0], 0, 72), AF.Copy)
+        tt(A("TS"), A(banks[1], 0, 72), A("TR", 0, 72), OP.min)
+        tt(A("TS", 0, 24), A("TS", 0, 24), A("TS", 48, 72), OP.min)
+        tt(A("TU", 0, 48), A(banks[2], 0, 48), A("TS", 0, 48), OP.min)
+        tt(A("TU", 48, 72), A("TU", 0, 24), A("TU", 24, 48), OP.min)
+        tt(out, A("TU", 48, 60), A("TU", 60, 72), OP.min)
+
+    def rows(banks, j, bmat, src, stop=False):
+        c0, c1 = (S2 if banks[1] == "pa" and PAR["s2"] else S4)[j]
+        for i in range(16):
+            mm(A(banks[j], 0, c1 - c0), A(bmat, 15 - i, 143 - i), A(src, 16 * c0 + i, 16 * c1, 16), False, stop and i == 15)
+
+    def least(banks, out, spare):
+        act(A("TR", 0, 96), A(banks[0], 0, 96), AF.Copy)
+        tt(A("TS"), A(banks[1], 0, 72), A("TR", 0, 72), OP.min)
+        tt(A("TU", 0, 24), A("TS", 0, 24), A("TS", 24, 48), OP.min)
+        tt(A("TU", 24, 48), A("TS", 48, 72), A("TR", 72, 96), OP.min)
+        if spare:
+            tt(A("TU", 0, 12), A("TU", 0, 12), A("TR", 96, 108), OP.min)
+        tt(A("TU", 48, 72), A("TU", 0, 24), A("TU", 24, 48), OP.min)
+        tt(A("TS", 0, 24), A(banks[2], 0, 24), A("TU", 48, 72), OP.min)
+        tt(out, A("TS", 0, 12), A("TS", 12, 24), OP.min)
+
+    def chunks(sizes):
+        k = 0
+        for s in sizes:
+            yield k, k + s
+            k += s
+
+    def codes(tn, out):
+        act(A("JJ"), A("XC"), AF.Relu, bias=-1024.0 * (128 + LIMS[tn]), scale=1024.0)
+        lin(A("py", 0, 384), [("I1", A("XC")), ("I1", A("JJ"))])
+        act(A(out), A("py", 0, 384), AF.Copy)
+
+    def pairs(b, own, slot, stop=False):
+        e = A("E", 384 * slot + 32 * b, 384 * slot + 384)
+        ts(e, A("L16", 32 * b, 384), A("nar", own + b, own + b + 1), OP.is_equal, A("WL", 16 * b + 15, 16 * b + 16), OP.mult)
+        mm(A("ph", 32 * b, 384), A("BO"), e, False, stop)
+
+    def scatter(win, ou, o0, o1, src, piece):
+        for c in range(0, o1 - o0, piece):
+            cp(ind(A(win), A(ou, o0 + c, o0 + c + piece)), A(src, 16 * c, 16 * (c + piece)))
+
+    wc, cc, f192, selr, f5, nb, c2, ty, c1y = [A("nar", 12 * k, 12 * k + 12) for k in range(9)]
+    K2, K4 = ("pk", "pa", "pb"), ("pk", "pz", "pu")
+    WU, CEU, SEL = A("WU"), A("CEU"), A("SEL")
+
+    for t in range(3):
+        NU, ZY, Gt, OU = "NU%d" % t, "ZY%d" % t, "G%d" % t, "OU%d" % (t % 2)
+        z, yw = A(ZY, 0, LN), A(ZY, LN, 384)
+        if t > 0:
+            ops.append({"q": "G", "f": None, "w": [A(NU), z], "r": [], "kind": "arr", "t": t, "cost": 0.0, "lat": 0.0})
+            cp(A("L"), A(NU))
+        for h in (0, 1):
+            mm(A("pz", LN * h, LN * h + LN), A("I1"), z, True, True)
+        for j, (c0, c1) in enumerate(S2 if PAR["s2"] else S4):
+            mm(A(K2[j], 0, c1 - c0), A("IF"), A("L", c0, c1), True, False)
+        if t == 0:
+            table0()
+        fixed(True)
+        for k0, k1 in chunks(PAR["ca"]):
+            act(A("ga", 384 * k0, 384 * k1), ind(A("Y", 0, NM), A(NU, 24 * k0, 24 * k1)), AF.Copy)
+        for k in range(8):
+            tt(A("ma", 384 * k, 384 * k + 384), A("ga", 384 * k, 384 * k + 384), A("pz", 0, 384), OP.max)
+            if k == 6:
+                behind("s2")
+        for j in range(3):
+            rows(K2, j, "Bp2", "ga")
+            rows(K2, j, "Bm4", "ma", True)
+        if PAR["s2"]:
+            least2(K2, A("K0"))
+        else:
+            least(K2, A("K0"), False)
+        ts(A("WI"), A("K0"), 2047, OP.bitwise_and)
+        cp(WU, A("WI"))
+        act(yw, ind(A("Y", 0, NM), WU), AF.Copy)
+        mm(A("pu", 0, LN), A("IF"), A("DG"), True, False)
+        mm(A("pu", 0, LN), A("BOh"), yw, False, False)
+        mm(A("pu", 0, LN), A("BOl"), yw, False, True)
+        act(A("GW", 0, LN), ind(A(Gt, 0, NM), WU), AF.Copy)
+        act(A("GW", LN, 384), ind(A(Gt, GS, GS + NM), WU), AF.Copy)
+        for h in (0, 1):
+            mm(A("pa", LN * h, LN * h + LN), A("I1"), A("GW", 0, LN), True, True)
+            mm(A("pb", LN * h, LN * h + LN), A("I1"), A("GW", LN, 384), True, True)
+        scan(A("ZS"), A("KP"), A("pu", 0, LN), 0.0, OP.mult, OP.max)
+        cp(A("U0"), A("ZS", 15, LN, 16))
+        ts(A("UI", 0, 12), A("U0"), 2047, OP.bitwise_and)
+        tt(A("USQ"), A("UI", 0, 12), A("UI", 0, 12), OP.mult)
+        ts(A("BS", 0, 12), A("USQ"), 1.0 / 32, OP.mult, A("AC"), OP.add)
+        for c0, c1 in PAR["cc"]:
+            rep = A("REP", c0 // 16, c1 // 16)
+            tt(A("KU", c0, c1), ind(A("UI", 0, 12), rep), A("KT", c0, c1), OP.mult)
+            tt(A("C0", c0, c1), ind(A("BS", 0, 12), rep), A("KU", c0, c1), OP.add)
+            ts(A("CI", c0, c1), A("C0", c0, c1), 2047, OP.bitwise_and)
+            cp(A("CU", c0, c1), A("CI", c0, c1))
+        fixed(False)
+        cp(A("WCU", 0, 24, 2), A("WI"))
+        lin(A("px", 0, LN), [("I1", z), ("Im1", yw)])
+        act(A("SZ%d" % t), A("px", 0, LN), AF.Abs)
+        ts(wc, A("WI"), -1024.0, OP.add)
+        ts(A("V0"), A("U0"), 1023, OP.bitwise_and)
+        ts(A("VF", 0, 12), A("V0"), 2.0, OP.mult, 33.0, OP.add)
+        tt(A("S7"), ind(A("VF", 0, 12), A("REP")), A("L"), OP.mult)
+        lin(A("py", 0, LN), [("IF", A("K32")), ("IF", A("S7"))])
+        cp(A("S8"), A("py", 0, LN))
+        ts(A("S9"), A("S8"), 5, OP.arith_shift_right, 2047, OP.bitwise_and)
+        if t < 2:
+            cp(A("SN%d" % t), A("S9"))
+            add("G", (lambda v: lambda: send(v))(t + 1), None, [A("SN%d" % t), A("SZ%d" % t)], kind="send", t=t + 1, cost=500.0)
+        else:
+            cp(A("D384"), ind(A("S9"), A("INV1")))
+            tr(A("T384"), A("D384"))
+            cp(A("S7"), ind(A("T384"), A("INV2")))
+            before("s4")
+            store("Y", T.yn[:, :], A("S7"))
+            store("Y", T.yz[:, :], A("SZ2"))
+        tt(A("M17"), A("pa", 0, LN), A("GW", LN, 384), OP.min)
+        for i in range(16):
+            mm(A("pu", 0, 12), A("Bp4", 15 - i, 143 - i), A("M17", i, LN, 16), i == 0, i == 15)
+        ts(f5, A("pu", 0, 12), 2600.0 * 4096, OP.is_ge, BIG, OP.mult)
+        ts(f192, f5, 192.0, OP.min)
+        tt(A("TR", 96, 108), f5, A("DT", 24, 36), OP.add)
+        tt(ty, f5, A("WI"), OP.add)
+        tt(selr, f192, lane, OP.add)
+        cp(SEL, selr)
+        ts(A("CT"), A("CI"), -4095.0 * 4096, OP.add)
+        for j, (c0, c1) in enumerate(S4):
+            mm(A(K4[j], 0, c1 - c0), A("IF"), A("CT", c0, c1), True, False)
+        na = PAR["na"]
+        fixed(True)
+        for k0, k1 in chunks(PAR["cb"]):
+            k0 = max(k0, na)
+            if k0 < k1:
+                off = A("CU", 24 * k0, 24 * k1)
+                act(A("ga", 384 * k0, 384 * k1), ind(A(Gt, GS, GS + NM), off), AF.Copy)
+                act(A("gb", 384 * k0, 384 * k1), ind(A(Gt, 0, NM), off), AF.Copy)
+        for m in range(2 * na):
+            off = A("CU", 12 * m, 12 * m + 12)
+            tt(A("ma", LN * m, LN * m + LN), ind(A(Gt, GS, GS + NM), off), A("GW", 0, LN), OP.min)
+            tt(A("mb", LN * m, LN * m + LN), ind(A(Gt, 0, NM), off), A("GW", LN, 384), OP.min)
+        for k in range(na, 8):
+            c = (384 * k, 384 * k + 384)
+            tt(A("ma", *c), A("ga", *c), A("pa", 0, 384), OP.min)
+            tt(A("mb", *c), A("gb", *c), A("pb", 0, 384), OP.min)
+        behind("s4")
+        for j in range(3):
+            rows(K4, j, "Bp4", "ma")
+            rows(K4, j, "Bp4", "mb", True)
+        least(K4, A("E0"), True)
+        ts(A("CE"), A("E0"), 4095, OP.bitwise_and)
+        fixed(False)
+        if t == 0:
+            table(1, PAR.get("q1", "VVVVVVVV"))
+            table(2, PAR.get("q2", "SSSSSSSS"))
+        if t == 0:
+            lin(A("ph", 0, 384), [("IF", A("TH")), ("IF", A("ZH"))])
+            act(A("TH"), A("ph", 0, 384), AF.Copy)
+        mm(A("ph", 0, 384), A("IF"), A("TH"), True, False)
+        fixed(True)
+        cp(A("WCU", 1, 24, 2), A("CE"))
+        cp(CEU, A("CE"))
+        cp(A("L16"), ind(A("LC"), A("WCU")))
+        ts(cc, A("CE"), -1024.0, OP.add)
+        for b in range(12):
+            pairs(b, 0, b)
+            pairs(b, 12, 12 + b, stop=(b == 11))
+        fixed(False)
+        act(A("PW", 0, LN), ind(A("P2", 0, NM), WU), AF.Copy)
+        act(A("PW", LN, 384), ind(A("P1", 0, NM), WU), AF.Copy)
+        act(A("WX", LN, 576), A("PW"), bias=RND, scale=1.0 / 16)
+        for h in (0, 1):
+            lin(A("px", LN * h, LN * h + LN),
+                [("I1", A("PW", LN * h, LN * h + LN)), ("Im1", z), ("Im16", A("WX", LN * h + LN, LN * h + 384))])
+        act(A("SG"), A("px", 0, 384), AF.Sign, bias=2064.0)
+        act(A("NE"), A("SG"), AF.Abs)
+        lin(A("py", 0, 384), [("I1", A("WX", LN, 576)), ("I1", A("NE"))])
+        act(A("RR"), A("py", 0, 384), AF.Relu, bias=144.0, scale=-1.0)
+        act(A("VV"), ind(A(ZY), SEL), AF.Copy)
+        lin(A("px", 0, LN), [("Im16", A("RR", 0, LN)), ("I1", z)])
+        lin(A("px", LN, 384), [("Im16", A("RR", LN, 384)), ("I1", z)])
+        lin(A("py", 0, LN), [("I16", A("WX", 384, 576)), ("I1", yw)])
+        act(A("P2", NM, NM + LN), A("px", 0, LN), bias=240.0)
+        act(A("SP", 0, LN), A("px", LN, 384), bias=240.0)
+        act(A("SP", LN, 384), A("py", 0, LN), bias=-2064.0)
+        act(A("VP1", 0, LN), ind(A("SP"), SEL), AF.Copy)
+        if t < 2:
+            act(A("WX", 0, LN), A("RR", LN, 384), bias=144.0, scale=-1.0)
+            act(A("XC", LN, 384), ind(A("WX", 0, 384), SEL), AF.Copy)
+        act(A("XC", 0, LN), ind(A("P2", 0, 2240), CEU), bias=RND, scale=1.0 / 16)
+        if t < 2:
+            codes(t + 1, "VG")
+        act(A("Y", NM, 2240), z, AF.Copy)
+        act(A("YC"), ind(A("Y", 0, 2240), CEU), AF.Copy)
+        act(A("WC"), ind(A("P1", 0, 2240), CEU), bias=RND, scale=1.0 / 16)
+        lin(A("px", 0, LN), [("I16", A("XC", 0, LN)), ("I1", A("VV"))])
+        lin(A("px", LN, 384), [("I16", A("WX", LN, 384)), ("I1", A("YC"))])
+        act(A("VP2"), A("px", 0, 384), bias=-2064.0)
+        lin(A("py", 0, LN), [("I16", A("WC")), ("I1", A("YC"))])
+        act(A("VP1", LN, 384), A("py", 0, LN), bias=-2064.0)
+        if t == 0:
+            codes(2, "VD")
+        ts(nb, A("E0"), 450.0 * 4096, OP.is_ge, BIG, OP.mult)
+        cp(A("TT", 24, 36), A("CE"))
+        tt(A("TT", 12, 24), nb, A("WI"), OP.add)
+        ts(c1y, A("CE"), 2240.0, OP.add)
+        tt(A("TT", 0, 12), c1y, ty, OP.min)
+        if t < 2:
+            ts(c2, A("CE"), float(GS), OP.add)
+            ts(A("TT", 36, 48), A("TT", 12, 24), float(GS), OP.add)
+            tt(A("TT", 48, 60), c2, ty, OP.min)
+        fixed(True)
+        scan(A("ZH"), A("KH"), A("ph", 0, 384), 0.0, OP.mult, OP.max)
+        ts(A("OA"), ind(A("ZH"), A("R16")), 0.0, OP.is_gt, BIG, OP.mult)
+        tt(A("OB"), A("OA"), A("TT"), OP.add)
+        tt(A("OF"), A("OB"), A("DT"), OP.min)
+        cp(A(OU), A("OF"))
+        if t < 2:
+            cp(ind(A("Y"), A(OU, 0, 12)), A("VP1", LN, 384))
+            fixed(False)
+            fill(A("P1", NM, 2240))
+            scatter("G%d" % (t + 1), OU, 36, 60, "VG", PAR["piece"])
+            before("s2")
+            add("S", lambda: S.activation(ap(A("EX", 0, 12)), ap(A("OF", 24, 36)), AF.Sign, bias=-2047.5, scale=1.0,
+                                          accum_out=ap(A("EX", 12, 13))), A("EX", 0, 13), [A("OF", 24, 36)])
+            mm(A("pu", 0, 1), A("ONE"), A("EX", 12, 13), True, True)
+            act(A("AC"), A("pu", 0, 1), bias=768.0 - 0.484375, scale=-0.5)
+            scatter("P2", OU, 12, 36, "VP2", PAR["piece"])
+            scatter("P1", OU, 12, 24, "VP1", PAR["piece"])
+            if t == 0:
+                scatter("G2", OU, 36, 60, "VD", PAR["piece"])
+                before("s4")
+        else:
+            scatter("P2", OU, 12, 36, "VP2", 24)
+            store("Y", T.ys[:, 0:1024], A("P2", 0, 1024))
+            store("S", T.ys[:, 1024:NM], A("P2", 1024, NM))
+            scatter("P1", OU, 12, 24, "VP1", 12)
+            cp(ind(A("Y"), A(OU, 0, 12)), A("VP1", LN, 384))
+            for k in range(32):
+                mm(A("px", 0, 64), A("I1"), A("P1", 64 * k, 64 * k + 64), k == 0, k == 31)
+            cp(A("YF"), A("px", 0, 64))
+            store("Y", T.yf[:, :], A("YF"))

@@ -19,13 +19,13 @@ def _decl(dtype, spec, where="sbuf"):
 
 
 _decl("bfloat16", "P2:2432 Y:4672 W:4096 G0:4864 G1:4864 G2:4864 ZY0:384 ZY1:384 ZY2:384 SZ0:192 SZ1:192 SZ2:192 "
-      "ga:3072 gb:3072 ma:3072 mb:3072 E:9216 I1:128 Im1:128 I16:128 Im16:128 Bp4:144 Bm4:144 Bp2:144 BO:128 BOh:128 "
-      "BOl:128 GW:384 M17:192 PW:384 WX:576 SG:384 NE:384 RR:384 JJ:384 SP:384 VV:192 VP1:384 VP2:384 VG:384 VD:384 "
+      "ga:3072 gb:3072 mx:3264 TH:576 DG:192 mb:3072 E:9216 I1:128 Im1:128 I16:128 Im16:128 Bp4:144 Bm4:144 Bp2:144 BO:128 BOh:128 "
+      "BOl:128 GW:384 PW:384 WX:576 SG:384 NE:384 RR:384 JJ:384 SP:384 VV:192 VP1:384 VP2:384 VG:384 VD:384 "
       "XC:384 WC:192 YC:192")
 _decl("float16", "L16:384")
 _decl("float32", "LC:2240 IF:128 ONE:128 X:144 X2:128 col:16 JX:12 t24:24 u24:24 t12:12 REPf:12 KT:192 K32:192 DM:192 DR:192 "
-      "TH:384 KH:384 ZH:384 UP:192 UQ:192 HF:192 ZR:192 WL:192 KP:192 DG:192 DT:64 TT:64 OA:64 OB:64 OF:64 L:192 D384:384 T384:384 ZS:192 "
-      "USQ:12 KU:192 CT:192 FB:12 VF:16 S7:192 nar:128 YF:64 WTT:32 TR:112 TS:72 TU:72")
+      "UP:192 UQ:192 HF:192 ZR:192 WL:192 KP:192 DT:64 TT:64 OA:64 OB:64 OF:64 L:192 D384:384 T384:384 ZS:192 "
+      "USQ:12 KU:192 CT:204 FB:12 VF:16 S7:192 nar:128 YF:64 WTT:32 TR:112 TS:72 TU:72")
 _decl("int32", "NI:192 IP:8 WI:24 U0:24 UI:16 BS:16 C0:192 CI:192 S8:192 S9:192 CE:24")
 _decl("uint16", "NU0:192 NU1:192 NU2:192 SN0:192 SN1:192 REP:12 R16:4 PERM:12 DUP:24 INV1:24 INV2:12 WU:36 CU:192 "
       "CEU:12 SEL:12 OU0:64 OU1:64")
@@ -33,11 +33,13 @@ _decl("float32", "pz:512 pk:512 pu:512 pa:512 pb:512 ph:512 px:512 py:512", "psu
 
 NDMA = 28
 SEMAPHORES = ["cP", "cV", "cS", "cG", "arr1", "arr2", "left1", "left2"] + ["d%d" % i for i in range(NDMA)]
-PAR = {"cy": 1.0, "g": 1.5, "sc": 3.5, "pe": 0.42, "wake": 70.0, "bw": 180.0, "hop": 8000.0, "rounds": 40,
-       "moves": 800, "mix": 0.0, "noise": 600.0, "seed": 4, "ca": (1, 2, 3, 1, 1), "cb": (1, 2, 2, 2, 1), "piece": 12, "na": 1,
+PAR = {"cy": 1.0, "g": 1.5, "sc": 3.5, "pe": 0.55, "wake": 110.0, "bw": 180.0, "hop": 8000.0, "rounds": 40,
+       "moves": 2000, "mix": 0.0, "noise": 600.0, "seed": 5, "ca": (1, 2, 1, 2, 1, 1), "piece": 12,
+       "cb": ((0, 1, 3), (1, 1, 3), (0, 3, 6), (1, 3, 6), (0, 6, 8), (1, 6, 7), (1, 7, 8)), "na": ((0, 0), (1, 0), (0, 1), (1, 1)),
        "q0": "VVVVVVVV", "q1": "SSSSSSSS", "q2": "VVVVSSSS", "qw": "VVVV", "s2": 1, "cc": ((0, 192),), "nd": 4}
 ORDER = {}
-PART = {"P1": ("Y", 2240, GS), "J0": ("mb", -1024, 4096), "WU": ("WU", 0, 12), "WCU": ("WU", 12, 24),
+PART = {"P1": ("Y", 2240, GS), "ma": ("mx", LN, 3072), "M17": ("mx", 0, LN),
+        "J0": ("mb", -1024, 4096), "WU": ("WU", 0, 12), "WCU": ("WU", 12, 24),
         "WH": ("IP", 4, 4), "K0": ("WI", 12, 12), "V0": ("U0", 12, 12), "E0": ("CE", 12, 12),
         "WI": ("WI", 0, 12), "U0": ("U0", 0, 12), "CE": ("CE", 0, 12), "EX": ("nar", 112, 16), "AC": ("col", 12, 1)}
 
@@ -487,14 +489,13 @@ def build(ops, T, g, send):
     scan(A("UP"), A("HF"), A("ZR"), 2.0 ** 96, OP.mult, OP.add)
     tt(A("UQ"), A("UP"), A("DM"), OP.mult)
     scan(A("WL"), A("KP"), A("UQ"), 0.0, OP.mult, OP.max)
-    iota(A("KH"), [[0, 12], [1, 32]])
-    iota(A("TH"), [[0, 24], [1, 16]])
-    ts(A("KH"), A("KH"), 0.0, OP.not_equal)
-    ts(A("TH"), A("TH"), rf, OP.not_equal, -2.0 ** 99, OP.mult)
-    ts(A("ZH"), ind(A("UQ"), A("DUP")), -2.5, OP.mult)
+    ts(A("TH", 0, LN), A("DR"), rf, OP.not_equal, -2.0 ** 99, OP.mult)
+    ts(A("TH", LN, 384), A("UQ"), -4.0, OP.mult)
+    ts(A("TH", 384, 576), A("UQ"), 2.0 ** -15, OP.mult)
+    fill(A("CT", 0, 12))
     for k, c in enumerate((2240 + 2048.0, 2240.0, 2048.0, GS + 2240.0, GS + 2048.0)):
         ts(A("DT", 12 * k, 12 * k + 12), lane, c, OP.add)
-    ts(A("R16"), A("REPf", 0, 4), 32.0, OP.mult, 31.0, OP.add)
+    ts(A("R16"), A("REPf", 0, 4), 16.0, OP.mult, 15.0, OP.add)
     ts(r12, rf, 12.0, OP.mult)
     ts(A("INV1"), A("u24"), r12, OP.add)
     cp(A("D384"), ind(A("NI"), A("DUP")))
@@ -554,31 +555,27 @@ def build(ops, T, g, send):
             else:
                 act(o, b, AF.Copy)
 
-    S2, S4 = ((0, 72), (72, 144), (144, 192)), ((0, 96), (96, 168), (168, 192))
+    SPLIT = ((0, 72), (72, 144), (144, 192))
 
-    def least2(banks, out):
-        act(A("TR", 0, 72), A(banks[0], 0, 72), AF.Copy)
+    def least(banks, out, spare):
+        act(A("TR", 0, 72), A(banks[0], 12, 84) if spare else A(banks[0], 0, 72), AF.Copy)
         tt(A("TS"), A(banks[1], 0, 72), A("TR", 0, 72), OP.min)
         tt(A("TS", 0, 24), A("TS", 0, 24), A("TS", 48, 72), OP.min)
+        if spare:
+            tt(A("TS", 24, 36), A("TS", 24, 36), A("TR", 96, 108), OP.min)
         tt(A("TU", 0, 48), A(banks[2], 0, 48), A("TS", 0, 48), OP.min)
         tt(A("TU", 48, 72), A("TU", 0, 24), A("TU", 24, 48), OP.min)
         tt(out, A("TU", 48, 60), A("TU", 60, 72), OP.min)
 
     def rows(banks, j, bmat, src, stop=False):
-        c0, c1 = (S2 if banks[1] == "pa" and PAR["s2"] else S4)[j]
+        c0, c1 = SPLIT[j]
         for i in range(16):
-            mm(A(banks[j], 0, c1 - c0), A(bmat, 15 - i, 143 - i), A(src, 16 * c0 + i, 16 * c1, 16), False, stop and i == 15)
-
-    def least(banks, out, spare):
-        act(A("TR", 0, 96), A(banks[0], 0, 96), AF.Copy)
-        tt(A("TS"), A(banks[1], 0, 72), A("TR", 0, 72), OP.min)
-        tt(A("TU", 0, 24), A("TS", 0, 24), A("TS", 24, 48), OP.min)
-        tt(A("TU", 24, 48), A("TS", 48, 72), A("TR", 72, 96), OP.min)
-        if spare:
-            tt(A("TU", 0, 12), A("TU", 0, 12), A("TR", 96, 108), OP.min)
-        tt(A("TU", 48, 72), A("TU", 0, 24), A("TU", 24, 48), OP.min)
-        tt(A("TS", 0, 24), A(banks[2], 0, 24), A("TU", 48, 72), OP.min)
-        tt(out, A("TS", 0, 12), A("TS", 12, 24), OP.min)
+            if banks[1] == "pz" and j == 0:
+                lead = 12 if src == "ma" else 0
+                o, r = A("pk", 12 - lead, 84), A(src, i - 16 * lead, 16 * c1, 16)
+            else:
+                o, r = A(banks[j], 0, c1 - c0), A(src, 16 * c0 + i, 16 * c1, 16)
+            mm(o, A(bmat, 15 - i, 143 - i), r, False, stop and i == 15)
 
     def chunks(sizes):
         k = 0
@@ -591,10 +588,11 @@ def build(ops, T, g, send):
         lin(A("py", 0, 384), [("I1", A("XC")), ("I1", A("JJ"))])
         act(A(out), A("py", 0, 384), AF.Copy)
 
-    def pairs(b, own, slot, stop=False):
-        e = A("E", 384 * slot + 32 * b, 384 * slot + 384)
-        ts(e, A("L16", 32 * b, 384), A("nar", own + b, own + b + 1), OP.is_equal, A("WL", 16 * b + 15, 16 * b + 16), OP.mult)
-        mm(A("ph", 32 * b, 384), A("BO"), e, False, stop)
+    def pairs(b, own, half, slot, stop=False):
+        e = A("E", LN * slot + 16 * b, LN * slot + LN)
+        ts(e, A("L16", LN * half + 16 * b, LN * half + LN), A("nar", own + b, own + b + 1), OP.is_equal,
+           A("WL", 16 * b + 15, 16 * b + 16), OP.mult)
+        mm(A("ph", 16 * b, LN), A("BO"), e, False, stop)
 
     def scatter(win, ou, o0, o1, src, piece):
         for c in range(0, o1 - o0, piece):
@@ -612,7 +610,7 @@ def build(ops, T, g, send):
             cp(A("L"), A(NU))
         for h in (0, 1):
             mm(A("pz", LN * h, LN * h + LN), A("I1"), z, True, True)
-        for j, (c0, c1) in enumerate(S2 if PAR["s2"] else S4):
+        for j, (c0, c1) in enumerate(SPLIT):
             mm(A(K2[j], 0, c1 - c0), A("IF"), A("L", c0, c1), True, False)
         if t == 0:
             table0()
@@ -626,14 +624,11 @@ def build(ops, T, g, send):
         for j in range(3):
             rows(K2, j, "Bp2", "ga")
             rows(K2, j, "Bm4", "ma", True)
-        if PAR["s2"]:
-            least2(K2, A("K0"))
-        else:
-            least(K2, A("K0"), False)
+        least(K2, A("K0"), False)
         ts(A("WI"), A("K0"), 2047, OP.bitwise_and)
         cp(WU, A("WI"))
         act(yw, ind(A("Y", 0, NM), WU), AF.Copy)
-        mm(A("pu", 0, LN), A("IF"), A("DG"), True, False)
+        mm(A("pu", 0, LN), A("I1"), A("DG"), True, False)
         mm(A("pu", 0, LN), A("BOh"), yw, False, False)
         mm(A("pu", 0, LN), A("BOl"), yw, False, True)
         act(A("GW", 0, LN), ind(A(Gt, 0, NM), WU), AF.Copy)
@@ -653,15 +648,13 @@ def build(ops, T, g, send):
             ts(A("CI", c0, c1), A("C0", c0, c1), 2047, OP.bitwise_and)
             cp(A("CU", c0, c1), A("CI", c0, c1))
         fixed(False)
-        cp(A("WCU", 0, 24, 2), A("WI"))
         lin(A("px", 0, LN), [("I1", z), ("Im1", yw)])
         act(A("SZ%d" % t), A("px", 0, LN), AF.Abs)
         ts(wc, A("WI"), -1024.0, OP.add)
         ts(A("V0"), A("U0"), 1023, OP.bitwise_and)
         ts(A("VF", 0, 12), A("V0"), 2.0, OP.mult, 33.0, OP.add)
         tt(A("S7"), ind(A("VF", 0, 12), A("REP")), A("L"), OP.mult)
-        lin(A("py", 0, LN), [("IF", A("K32")), ("IF", A("S7"))])
-        cp(A("S8"), A("py", 0, LN))
+        tt(A("S8"), A("S7"), A("K32"), OP.add)
         ts(A("S9"), A("S8"), 5, OP.arith_shift_right, 2047, OP.bitwise_and)
         if t < 2:
             cp(A("SN%d" % t), A("S9"))
@@ -674,55 +667,52 @@ def build(ops, T, g, send):
             store("Y", T.yn[:, :], A("S7"))
             store("Y", T.yz[:, :], A("SZ2"))
         tt(A("M17"), A("pa", 0, LN), A("GW", LN, 384), OP.min)
-        for i in range(16):
-            mm(A("pu", 0, 12), A("Bp4", 15 - i, 143 - i), A("M17", i, LN, 16), i == 0, i == 15)
-        ts(f5, A("pu", 0, 12), 2600.0 * 4096, OP.is_ge, BIG, OP.mult)
+        ts(A("CT", 12, 204), A("CI"), -4095.0 * 4096, OP.add)
+        for j, (c0, c1) in enumerate(((0, 84), (84, 156), (156, 204))):
+            mm(A(K4[j], 0, c1 - c0), A("IF"), A("CT", c0, c1), True, False)
+        na = PAR["na"]
+        fixed(True)
+        pages = (("ga", "ma", "pa", A(Gt, GS, GS + NM), A("GW", 0, LN)), ("gb", "mb", "pb", A(Gt, 0, NM), A("GW", LN, 384)))
+        for h, m in na:
+            got, low, own, win, gw = pages[h]
+            tt(A(low, LN * m, LN * m + LN), ind(win, A("CU", 12 * m, 12 * m + 12)), gw, OP.min)
+        for h, k0, k1 in PAR["cb"]:
+            got, low, own, win, gw = pages[h]
+            act(A(got, 384 * k0, 384 * k1), ind(win, A("CU", 24 * k0, 24 * k1)), AF.Copy)
+            for k in range(k0, k1):
+                tt(A(low, 384 * k, 384 * k + 384), A(got, 384 * k, 384 * k + 384), A(own, 0, 384), OP.min)
+        behind("s4")
+        for j in range(3):
+            rows(K4, j, "Bp4", "ma")
+            rows(K4, j, "Bp4", "mb", True)
+        fixed(False)
+        ts(f5, A("pk", 0, 12), 2600.0 * 4096, OP.is_ge, BIG, OP.mult)
         ts(f192, f5, 192.0, OP.min)
         tt(A("TR", 96, 108), f5, A("DT", 24, 36), OP.add)
         tt(ty, f5, A("WI"), OP.add)
         tt(selr, f192, lane, OP.add)
         cp(SEL, selr)
-        ts(A("CT"), A("CI"), -4095.0 * 4096, OP.add)
-        for j, (c0, c1) in enumerate(S4):
-            mm(A(K4[j], 0, c1 - c0), A("IF"), A("CT", c0, c1), True, False)
-        na = PAR["na"]
         fixed(True)
-        for k0, k1 in chunks(PAR["cb"]):
-            k0 = max(k0, na)
-            if k0 < k1:
-                off = A("CU", 24 * k0, 24 * k1)
-                act(A("ga", 384 * k0, 384 * k1), ind(A(Gt, GS, GS + NM), off), AF.Copy)
-                act(A("gb", 384 * k0, 384 * k1), ind(A(Gt, 0, NM), off), AF.Copy)
-        for m in range(2 * na):
-            off = A("CU", 12 * m, 12 * m + 12)
-            tt(A("ma", LN * m, LN * m + LN), ind(A(Gt, GS, GS + NM), off), A("GW", 0, LN), OP.min)
-            tt(A("mb", LN * m, LN * m + LN), ind(A(Gt, 0, NM), off), A("GW", LN, 384), OP.min)
-        for k in range(na, 8):
-            c = (384 * k, 384 * k + 384)
-            tt(A("ma", *c), A("ga", *c), A("pa", 0, 384), OP.min)
-            tt(A("mb", *c), A("gb", *c), A("pb", 0, 384), OP.min)
-        behind("s4")
-        for j in range(3):
-            rows(K4, j, "Bp4", "ma")
-            rows(K4, j, "Bp4", "mb", True)
         least(K4, A("E0"), True)
         ts(A("CE"), A("E0"), 4095, OP.bitwise_and)
         fixed(False)
         if t == 0:
             table(1, PAR.get("q1", "VVVVVVVV"))
             table(2, PAR.get("q2", "SSSSSSSS"))
-        if t == 0:
-            lin(A("ph", 0, 384), [("IF", A("TH")), ("IF", A("ZH"))])
-            act(A("TH"), A("ph", 0, 384), AF.Copy)
-        mm(A("ph", 0, 384), A("IF"), A("TH"), True, False)
-        fixed(True)
-        cp(A("WCU", 1, 24, 2), A("CE"))
-        cp(CEU, A("CE"))
-        cp(A("L16"), ind(A("LC"), A("WCU")))
-        ts(cc, A("CE"), -1024.0, OP.add)
+        for k in range(3):
+            mm(A("ph", 0, LN), A("I1"), A("TH", LN * k, LN * k + LN), k == 0, False)
+        fixed(False)
+        cp(A("L16", 0, LN), ind(A("LC"), WU))
         for b in range(12):
-            pairs(b, 0, b)
-            pairs(b, 12, 12 + b, stop=(b == 11))
+            pairs(b, 0, 0, b)
+        fixed(True)
+        cp(CEU, A("CE"))
+        ts(cc, A("CE"), -1024.0, OP.add)
+        cp(A("L16", LN, 384), ind(A("LC"), CEU))
+        for b in range(12):
+            pairs(b, 12, 0, 12 + b)
+            pairs(b, 0, 1, 24 + b)
+            pairs(b, 12, 1, 36 + b, stop=(b == 11))
         fixed(False)
         act(A("PW", 0, LN), ind(A("P2", 0, NM), WU), AF.Copy)
         act(A("PW", LN, 384), ind(A("P1", 0, NM), WU), AF.Copy)
@@ -768,8 +758,8 @@ def build(ops, T, g, send):
             ts(A("TT", 36, 48), A("TT", 12, 24), float(GS), OP.add)
             tt(A("TT", 48, 60), c2, ty, OP.min)
         fixed(True)
-        scan(A("ZH"), A("KH"), A("ph", 0, 384), 0.0, OP.mult, OP.max)
-        ts(A("OA"), ind(A("ZH"), A("R16")), 0.0, OP.is_gt, BIG, OP.mult)
+        scan(A("ZS"), A("KP"), A("ph", 0, LN), 0.0, OP.mult, OP.max)
+        ts(A("OA"), ind(A("ZS"), A("R16")), 0.0, OP.is_gt, BIG, OP.mult)
         tt(A("OB"), A("OA"), A("TT"), OP.add)
         tt(A("OF"), A("OB"), A("DT"), OP.min)
         cp(A(OU), A("OF"))
@@ -792,8 +782,9 @@ def build(ops, T, g, send):
             scatter("P2", OU, 12, 36, "VP2", 24)
             store("Y", T.ys[:, 0:1024], A("P2", 0, 1024))
             store("S", T.ys[:, 1024:NM], A("P2", 1024, NM))
-            scatter("P1", OU, 12, 24, "VP1", 12)
-            cp(ind(A("Y"), A(OU, 0, 12)), A("VP1", LN, 384))
+            ts(A("OU1", 0, 12), A("OF", 12, 24), 2240.0, OP.add)
+            cp(A("OU1", 12, 24), A("OF", 0, 12))
+            cp(ind(A("Y"), A("OU1", 0, 24)), A("VP1"))
             for k in range(32):
                 mm(A("px", 0, 64), A("I1"), A("P1", 64 * k, 64 * k + 64), k == 0, k == 31)
             cp(A("YF"), A("px", 0, 64))

from concourse.bass import DstId, RemoteDMATransfer
from concourse.mybir import AluOpType as OP, AxisListType as AX, ActivationFunctionType as AF

NM, LN = 2048, 192
LIMS = (13, 10, 12)
WT = (1, 16, 256, 37, 411, 93, 777, 165, 1029, 251, 1313, 339, 1583, 503, 1847, 618)
KA = (3, 61, 118, 207, 346, 419, 530, 677, 742, 895, 1011, 1164, 1283, 1450, 1629, 1874)
GS = 2432
BIG = 2048000.0
RND = 128.53125

SCRATCH = {}


def _decl(dtype, spec, where="sbuf"):
    for item in spec.split():
        name, n = item.split(":")
        SCRATCH[name] = (where, [128, int(n)], dtype)


_decl("bfloat16", "P2:2432 Y:4672 W:4096 G0:4864 G1:4864 G2:4864 ZY0:384 ZY1:384 ZY2:384 SZ0:192 SZ1:192 SZ2:192 "
      "ga:3072 gb:3072 mx:3264 TH:576 DG:192 mb:3072 E:9216 I1:128 Im1:128 I16:128 Im16:128 Bp4:144 Bm4:144 Bp2:144 BO:128 BOh:128 "
      "BOl:128 GW:384 PW:384 WX:576 SG:384 NE:384 RR:384 JJ:384 SP:384 VV:192 VP1:384 VP2:384 VG:384 VD:384 "
      "XC:384 WC:192 YC:192")
_decl("float16", "L16:384")
_decl("float32", "LC:2240 IF:128 ONE:128 X:144 X2:128 col:16 JX:12 t24:24 u24:24 t12:12 REPf:12 KT:192 K32:192 DM:192 DR:192 "
      "UP:192 UQ:192 HF:192 ZR:192 WL:192 KP:192 DT:64 TT:64 OA:64 OB:64 OF:64 L:192 D384:384 T384:384 ZS:192 "
      "USQ:12 KU:192 CT:204 FB:12 VF:16 S7:192 nar:128 YF:64 WTT:32 TR:112 TS:72 TU:72")
_decl("int32", "NI:192 IP:8 WI:24 U0:24 UI:16 BS:16 C0:192 CI:192 S8:192 S9:192 CE:24")
_decl("uint16", "NU0:192 NU1:192 NU2:192 SN0:192 SN1:192 REP:12 R16:4 PERM:12 DUP:24 INV1:24 INV2:12 WU:36 CU:192 "
      "CEU:12 SEL:12 OU0:64 OU1:64")
_decl("float32", "pz:512 pk:512 pu:512 pa:512 pb:512 ph:512 px:512 py:512", "psum")

NDMA = 28
SEMAPHORES = ["cP", "cV", "cS", "cG", "arr1", "arr2", "left1", "left2"] + ["d%d" % i for i in range(NDMA)]
PAR = {"cy": 1.0, "g": 1.5, "sc": 3.5, "pe": 0.55, "wake": 110.0, "bw": 180.0, "hop": 8000.0, "rounds": 40,
       "moves": 2000, "mix": 0.0, "noise": 600.0, "seed": 5, "ca": (1, 2, 1, 2, 1, 1), "piece": 12,
       "cb": ((0, 1, 3), (1, 1, 3), (0, 3, 6), (1, 3, 6), (0, 6, 8), (1, 6, 7), (1, 7, 8)), "na": ((0, 0), (1, 0), (0, 1), (1, 1)),
       "q0": "VVVVVVVV", "q1": "SSSSSSSS", "q2": "VVVVSSSS", "qw": "VVVV", "s2": 1, "cc": ((0, 192),), "nd": 4}
ORDER = {}
PART = {"P1": ("Y", 2240, GS), "ma": ("mx", LN, 3072), "M17": ("mx", 0, LN),
        "J0": ("mb", -1024, 4096), "WU": ("WU", 0, 12), "WCU": ("WU", 12, 24),
        "WH": ("IP", 4, 4), "K0": ("WI", 12, 12), "V0": ("U0", 12, 12), "E0": ("CE", 12, 12),
        "WI": ("WI", 0, 12), "U0": ("U0", 0, 12), "CE": ("CE", 0, 12), "EX": ("nar", 112, 16), "AC": ("col", 12, 1)}


def A(name, c0=0, c1=None, step=1):
    if name in PART:
        name, at, n = PART[name]
        return (name, at + c0, at + (n if c1 is None else c1), step)
    if c1 is None:
        c1 = SCRATCH[name][1][1]
    return (name, c0, c1, step)


def _overlap(a, b):
    if a[1] >= b[2] or b[1] >= a[2]:
        return False
    if a[3] == b[3] and a[3] > 1:
        return (a[1] - b[1]) % a[3] == 0
    return True


def _relay(src, dst, T, topo):
    if topo.may_write(src, dst):
        return None
    free = [c for c in topo.cores_of(src) if c != src and T.rank_of(c) is None and topo.may_write(c, dst)]
    near = [c for c in free if topo.die(c) == topo.die(src)]
    return (near or free)[0]


def _send(g, T, topo, src, dst, t, names, vec):
    eng = topo.engines(src, dst)
    half = len(eng) // 2
    rid, pid = topo.addr(dst, src)
    sem = T.sem["arr%d" % t]
    trs = []
    for part, s, d in ((eng[:half], names, T["NU%d" % t][:, 0:LN]), (eng[half:2 * half], vec, T["ZY%d" % t][:, 0:LN])):
        trs.append(RemoteDMATransfer(dst_ids=[DstId(rid=rid, pnc=pid)], dma_engine_mask=sum(1 << e for e in part),
                                     remote_sem=sem, src=s, dst=d))
    g.remote_dma_fused(trs, local_sem=T.sem["left%d" % t])
    return 2 * half


def _count(src, dst, topo):
    return 2 * (len(topo.engines(src, dst)) // 2)


def rank_program(g, core, T, topo):
    cores = list(T.cores)
    n = len(cores)
    rank = T.rank_of(core)
    if rank is None:
        for r in range(n):
            dst = cores[(r + 1) % n]
            if _relay(cores[r], dst, T, topo) == core:
                for t in (1, 2):
                    g.wait_ge(T.sem["arr%d" % t], _count(cores[r], core, topo))
                    k = _send(g, T, topo, core, dst, t, T["NU%d" % t][:, 0:LN], T["ZY%d" % t][:, 0:LN])
                for t in (1, 2):
                    g.wait_ge(T.sem["left%d" % t], k)
        return
    nxt, prv = cores[(rank + 1) % n], cores[(rank - 1) % n]
    hop = _relay(core, nxt, T, topo)
    hop = nxt if hop is None else hop
    frm = _relay(prv, core, T, topo)
    frm = prv if frm is None else frm
    ops = []
    build(ops, T, g, lambda t: _send(g, T, topo, core, hop, t, T["SN%d" % (t - 1)][:, 0:LN], T["SZ%d" % (t - 1)][:, 0:LN]))
    if "order" not in ORDER:
        ORDER["deps"], soft = hazards(ops)
        ORDER["order"] = schedule(ops, ORDER["deps"], soft)
    emit(ops, ORDER["deps"], ORDER["order"], T, g, _count(frm, core, topo), _count(core, hop, topo))


def hazards(ops):
    hist, deps, soft, sends = {}, [], [], {}
    for k, o in enumerate(ops):
        d, s = set(), set()
        accs = [(a, False) for a in o["r"]] + [(a, True) for a in o["w"]]
        for acc, wr in accs:
            psum = SCRATCH[acc[0]][0] == "psum"
            for j, b, bw in hist.get(acc[0], ()):
                same = ops[j]["q"] == o["q"] and ops[j]["kind"] == "c" and o["kind"] == "c"
                if same and o["q"] == "P":
                    if psum:
                        s.add(j)
                elif (psum and not same) or ((wr or bw) and _overlap(acc, b)):
                    d.add(j)
        for acc, wr in accs:
            h = hist.setdefault(acc[0], [])
            if SCRATCH[acc[0]][0] == "psum":
                if o["q"] == "P":
                    h[:] = []
            elif wr and acc[3] == 1:
                h[:] = [e for e in h if not (acc[1] <= e[1][1] and e[1][2] <= acc[2])]
            h.append((k, acc, wr))
        s.update(o.get("after", ()))
        if o["kind"] == "send":
            sends[o["t"]] = k
        if o["kind"] == "arr":
            s.add(sends[o["t"]])
        deps.append(d)
        soft.append(s)
    return deps, soft


def schedule(ops, deps, soft):
    n = len(ops)
    cost = [o["cost"] for o in ops]
    fwd = [[] for _ in range(n)]
    bwd = [[] for _ in range(n)]
    for k in range(n):
        for j in sorted(deps[k] | soft[k]):
            if j in deps[k]:
                gap = cost[j] + ops[j]["lat"] + PAR["wake"]
            else:
                gap = cost[j] + (PAR["hop"] if ops[k]["kind"] == "arr" else 0.0)
            fwd[j].append((k, gap))
            bwd[k].append((j, gap + cost[k] - cost[j]))

    def place(succ, pred, ready, prio, wires):
        left = [len(p) for p in pred]
        cand = [k for k in range(n) if left[k] == 0]
        busy = {q: [] for q in "PVSGY"}
        start, end = [0.0] * n, 0.0
        wire = []
        while cand:
            c = max(cand, key=lambda k: (prio[k], -k))
            cand.remove(c)
            line, t = busy[ops[c]["q"]], ready[c]
            lo, hi = 0, len(line)
            while lo < hi:
                mid = (lo + hi) // 2
                if line[mid][1] <= t:
                    lo = mid + 1
                else:
                    hi = mid
            while lo < len(line) and line[lo][0] < t + cost[c]:
                t = max(t, line[lo][1])
                lo += 1
            line.insert(lo, (t, t + cost[c]))
            start[c] = t
            extra = 0.0
            if wires and ops[c]["kind"] in ("d", "send"):
                w0, d = t + cost[c] + 1500.0, max(ops[c]["lat"] - 1500.0, 600.0)
                w = max([w0] + [y for x, y in wire if x <= t])
                wire.append((t, w + d))
                extra = w - w0
            end = max(end, t + cost[c] + ops[c]["lat"] + extra)
            for k, gap in succ[c]:
                ready[k] = max(ready[k], t + gap + (extra if gap > cost[c] + 1 else 0.0))
                left[k] -= 1
                if left[k] == 0:
                    cand.append(k)
        return start, end

    prio = [0.0] * n
    for j in reversed(range(n)):
        prio[j] = max([cost[j] + ops[j]["lat"]] + [gap + prio[k] for k, gap in fwd[j]])
    best, seed = None, PAR["seed"]
    for r in range(PAR["rounds"]):
        for k in range(n):
            if ops[k]["kind"] == "d" and not ops[k]["r"]:
                prio[k] = 1e9 - k
        st, end = place(fwd, bwd, [0.0] * n, prio, True)
        if best is None or end < best[0]:
            best = (end, st)
        if r % 2:
            st = best[1]
        back = place(bwd, fwd, [o["lat"] for o in ops], [st[k] + cost[k] for k in range(n)], False)[0]
        prio = []
        for k in range(n):
            seed = (seed * 1103515245 + 12345) % 2147483648
            mix = PAR["mix"] * (best[0] - best[1][k]) + (1 - PAR["mix"]) * (back[k] + cost[k])
            prio.append(mix + PAR["noise"] * seed / 2147483648.0)
    for r in range(PAR["moves"]):
        st = best[1]
        if r == 0 or fresh:
            prev, last = {}, {}
            for k in sorted(range(n), key=lambda k: st[k]):
                prev[k] = last.get(ops[k]["q"])
                last[ops[k]["q"]] = k
            k, held = max(range(n), key=lambda k: st[k] + cost[k] + ops[k]["lat"]), []
            while k is not None:
                j = prev[k]
                if j is not None and st[j] + cost[j] >= st[k] - 1 and j not in soft[k]:
                    held.append((j, k))
                    k = j
                else:
                    k = max((j for j, gap in bwd[k]), key=lambda j: st[j] + cost[j] + ops[j]["lat"], default=None)
        seed = (seed * 1103515245 + 12345) % 2147483648
        j, k = held[(seed >> 8) % len(held)]
        seed = (seed * 1103515245 + 12345) % 2147483648
        prio = [-s for s in st]
        step = 100.0 * 1.5 ** ((seed >> 8) % 12)
        if (seed >> 20) % 3 == 2:
            prio[j] -= step + cost[k]
        else:
            todo = [k if (seed >> 20) % 3 == 0 else j]
            prio[todo[0]] = prio[j] + step
            while todo:
                c = todo.pop()
                for a, gap in bwd[c]:
                    want = prio[c] + gap + cost[a] - cost[c]
                    if prio[a] < want - 1:
                        prio[a] = want
                        todo.append(a)
        new, end = place(fwd, bwd, [0.0] * n, prio, True)
        fresh = end <= best[0]
        if fresh:
            best = (end, new)
    ORDER["end"] = best[0]
    return sorted(range(n), key=lambda k: (best[1][k], k))


def emit(ops, deps, order, T, g, n_arr, n_left):
    queue = {"P": g.tensor, "V": g.vector, "S": g.scalar, "G": g, "Y": g.sync}
    pos = {k: i for i, k in enumerate(order)}
    seen = {q: {} for q in queue}
    need, keep = set(), {}
    for k in order:
        o = ops[k]
        last_p = max([pos[j] for j in deps[k] if ops[j]["q"] == "P"], default=-1)
        kd = [j for j in deps[k] if (ops[j]["q"] != "P" or pos[j] == last_p) and
              not (ops[j]["kind"] == "c" and seen[o["q"]].get(ops[j]["q"], -1) >= pos[j])]
        need.update(kd)
        for j in kd:
            if ops[j]["kind"] == "c":
                seen[o["q"]][ops[j]["q"]] = max(seen[o["q"]].get(ops[j]["q"], -1), pos[j])
        keep[k] = kd
    cnt = {q: 0 for q in "PVSG"}
    mark, total, ndma = {}, {}, 0
    waited = {q: {} for q in queue}
    for k in order:
        o = ops[k]
        want = {}
        for j in keep[k]:
            s, v = mark[j]
            want[s] = max(want.get(s, 0), v)
        for s, v in sorted(want.items()):
            if waited[o["q"]].get(s, 0) < v:
                queue[o["q"]].wait_ge(T.sem[s], v)
                waited[o["q"]][s] = v
        if o["kind"] == "arr":
            mark[k] = ("arr%d" % o["t"], n_arr)
            total[mark[k][0]] = n_arr
            continue
        ins = o["f"]()
        if o["kind"] == "send":
            total["left%d" % o["t"]] = n_left
        elif o["kind"] == "d":
            s = "d%d" % ndma
            ndma += 1
            ins.then_inc(T.sem[s], 16)
            mark[k] = (s, 16)
            total[s] = 16
        elif k in need:
            cnt[o["q"]] += 1
            ins.then_inc(T.sem["c" + o["q"]], 1)
            mark[k] = ("c" + o["q"], cnt[o["q"]])
            total["c" + o["q"]] = cnt[o["q"]]
    for s, v in sorted(total.items()):
        if max(w.get(s, 0) for w in waited.values()) < v:
            g.wait_ge(T.sem[s], v)


def build(ops, T, g, send):
    V, S, PE = g.vector, g.scalar, g.tensor
    size = {"bfloat16": 2, "float16": 2, "uint16": 2, "float32": 4, "int32": 4}

    def ap(a):
        if a[0] == "ind":
            return ap(a[1]).indirect(ap(a[2]))
        if a[3] == 1:
            return T[a[0]][:, a[1]:a[2]]
        return T[a[0]][:, a[1]:a[2]:a[3]]

    def width(a):
        return 16 * width(a[2]) if a[0] == "ind" else len(range(a[1], a[2], a[3]))

    def add(q, f, w, r, k=1.0, kind="c", t=0, cost=None, lat=0.0):
        rs = []
        for a in r:
            if isinstance(a, tuple):
                rs += [a[1], a[2]] if a[0] == "ind" else [a]
        if cost is None:
            if w[0] == "ind":
                cost = 50 + width(w) * PAR["sc"] * PAR["cy"]
            elif r and r[0][0] == "ind":
                cost = 50 + width(w) * PAR["g"] * PAR["cy"]
            else:
                cost = max(64, width(r[0] if r else w) * k) * PAR["cy"]
            cost += 15 if q == "S" else 0
        if w is not None and w[0] == "ind":
            rs.append(w[2])
            w = w[1]
        ops.append({"q": q, "f": f, "w": [] if w is None else [w], "r": rs, "kind": kind, "t": t, "cost": cost, "lat": lat})
        if spine["on"] and q in "VS" and kind == "c":
            ops[-1]["after"] = [spine[q]] if q in spine else []
            spine[q] = len(ops) - 1

    spine = {"on": False}

    def fixed(on):
        spine["on"] = on

    def val(x):
        return ap(x) if isinstance(x, tuple) else x

    def ind(win, off):
        return ("ind", win, off)

    def two(o, a):
        return 0.5 if "ind" not in (o[0], a[0]) and size[SCRATCH[o[0]][2]] == 2 and size[SCRATCH[a[0]][2]] == 2 else 1.0

    def cp(o, i):
        add("V", lambda: V.tensor_copy(ap(o), ap(i)), o, [i], two(o, i))

    def tt(o, a, b, op):
        k = 1.0 if a[0] == "ind" or "psum" in (SCRATCH[a[0]][0], SCRATCH[b[0]][0]) else 2.0
        add("V", lambda: V.tensor_tensor(ap(o), ap(a), ap(b), op), o, [a, b], k)

    def ts(o, a, s1, op0, s2=None, op1=None):
        if op1 is None:
            add("V", lambda: V.tensor_scalar(ap(o), ap(a), val(s1), None, op0), o, [a, s1], two(o, a))
        else:
            add("V", lambda: V.tensor_scalar(ap(o), ap(a), val(s1), val(s2), op0, op1), o, [a, s1, s2], two(o, a))

    def red(o, a, op):
        add("V", lambda: V.tensor_reduce(ap(o), ap(a), AX.X, op), o, [a])

    def scan(o, a, b, init, op0, op1):
        add("V", lambda: V.tensor_tensor_scan(ap(o), ap(a), ap(b), init, op0, op1), o, [a, b])

    def tr(o, a):
        add("V", lambda: V.transpose(ap(o), ap(a)), o, [a])

    def ms(o, c):
        add("V", lambda: V.memset(ap(o), c), o, [])

    def act(o, a, func=AF.Identity, bias=0.0, scale=1.0):
        add("S", lambda: S.activation(ap(o), ap(a), func, bias=bias, scale=scale), o, [a])

    def mm(o, l, r, start, stop):
        add("P", lambda: PE.matmul(ap(o), ap(l), ap(r), start, stop), o, [l, r],
            cost=max(64, width(r)) * PAR["pe"] * (4 if size[SCRATCH[l[0]][2]] == 4 else 1), lat=100.0)

    def lin(o, terms):
        for k, (l, r) in enumerate(terms):
            mm(o, A(l), r, k == 0, k == len(terms) - 1)

    def iota(o, pat, base=0, ch=0):
        cost = 130 + 2 * width(o) * PAR["cy"]
        if SCRATCH[o[0]][2] == "int32":
            add("G", lambda: g.iota(ap(o), pat, base, ch), o, [], cost=cost)
        else:
            add("G", lambda: g.iota(ap(o), pat, base, ch, allow_small_or_imprecise_dtypes=True), o, [], cost=cost)

    def fill(o, c=0):
        iota(o, [[0, width(o)]], c)

    def wire(a, k=1):
        return 1500.0 + k * 128 * width(a) * size[SCRATCH[a[0]][2]] / PAR["bw"]

    def load(q, o, src):
        add(q, lambda: {"Y": g.sync, "S": g.scalar}[q].dma_start(ap(o), src), o, [], kind="d", cost=100.0, lat=wire(o))

    def store(q, dst, i):
        add(q, lambda: {"Y": g.sync, "S": g.scalar}[q].dma_start(dst, ap(i)), None, [i], kind="d", cost=100.0, lat=wire(i))

    def dadd(o, i):
        add("G", lambda: g.dma_start(ap(o), ap(i), accum_op=OP.add), o, [i, o], kind="d", cost=500.0, lat=wire(o, 2))

    pf, rf, p31, g16, g15, c16, r12, r16, whi, wlo, wt = [A("col", k, k + 1) for k in range(11)]
    lane = A("JX")

    load("Y", A("NI"), T.nm[:, :])
    for k in range(4):
        load("S", A("P2", 512 * k, 512 * k + 512), T.pg[:, NM + 512 * k:NM + 512 * k + 512])
        load("Y", A("P1", 512 * k, 512 * k + 512), T.pg[:, 512 * k:512 * k + 512])
    load("S", A("ZY0", 0, LN), T.zv[:, :])
    for k in range(1, len(ops)):
        ops[k]["after"] = [k - 1]
    due = {}

    def before(tag):
        due.setdefault(tag, []).append(len(ops) - 1)

    def behind(tag):
        ops[-1]["after"] = ops[-1].get("after", []) + due.pop(tag, [])

    iota(A("IP", 0, 1), [[0, 1]], 0, 1)
    iota(A("FB"), [[16, 12]])
    iota(A("t24"), [[16, 12], [0, 2]])
    iota(A("u24"), [[1, 12], [0, 2]])
    iota(A("X"), [[1, 144]])
    iota(A("X2"), [[16, 8], [0, 16]])
    iota(A("DR"), [[0, 12], [1, 16]])
    iota(A("K32"), [[1, 16], [256, 12]])
    iota(A("LC"), [[1, 2240]], -1024)
    for m in range(16):
        iota(A("WTT", m, m + 1), [[0, 1]], WT[m])
        iota(A("KT", 12 * m, 12 * m + 12), [[0, 12]], KA[m])
    for a in (A("P1", NM, GS), A("P2", NM, GS), A("ZR"), A("DT", 60, 64), A("TT", 60, 64)):
        fill(a)
    for name in ("G1", "G2"):
        fill(A(name, NM, GS))
        fill(A(name, GS + NM, 2 * GS))
    fill(A("ONE"), 1)
    cp(pf, A("IP", 0, 1))
    ts(A("IP", 1, 2), A("IP", 0, 1), 15, OP.bitwise_and)
    ts(A("IP", 2, 3), A("IP", 0, 1), 31, OP.bitwise_and)
    cp(rf, A("IP", 1, 2))
    cp(p31, A("IP", 2, 3))
    ts(A("INV2"), A("FB"), 2.0, OP.mult, p31, OP.add)
    ts(A("DUP"), A("t24"), rf, OP.add)
    ts(lane, A("FB"), rf, OP.add)
    tt(c16, p31, rf, OP.subtract)
    tt(g16, pf, rf, OP.subtract)
    ts(A("K0"), lane, 1.0 / 12, OP.mult, -0.458, OP.add)
    for name, c in (("I1", 1.0), ("Im1", -1.0), ("Im16", -16.0), ("I16", 16.0), ("IF", 1.0)):
        ts(A(name), A("X", 0, 128), pf, OP.is_equal, c, OP.mult)
    ts(A("t12"), A("K0"), -12.0, OP.mult)
    ts(g15, g16, 15.0, OP.add)
    tt(A("REPf"), A("t12"), lane, OP.add)
    ts(A("t12"), A("REPf"), 32.0, OP.mult, c16, OP.add)
    tt(A("t12"), A("t12"), A("K0"), OP.add)
    cp(A("PERM"), A("t12"))
    cp(A("REP"), A("REPf"))
    for name, c in (("Bp2", 2048.0), ("Bm4", -4096.0), ("Bp4", 4096.0)):
        ts(A(name), A("X"), g15, OP.is_equal, c, OP.mult)
    ts(A("KP"), A("DR"), 0.0, OP.not_equal)
    ts(A("DM"), A("DR"), rf, OP.is_equal)
    ts(A("DG"), A("DR"), rf, OP.is_equal, 262144.0, OP.mult)
    ts(A("BO"), A("X2"), g16, OP.is_equal)
    tt(A("WTT", 16, 32), A("WTT", 0, 16), A("DM", 0, 16), OP.mult)
    red(wt, A("WTT", 16, 32), OP.add)
    cp(A("WH", 0, 1), wt)
    ts(A("WH", 1, 2), A("WH", 0, 1), 15, OP.bitwise_and)
    cp(wlo, A("WH", 1, 2))
    tt(whi, wt, wlo, OP.subtract)
    ts(A("BOl"), A("X2"), g16, OP.is_equal, wlo, OP.mult)
    ts(A("BOh"), A("X2"), g16, OP.is_equal, whi, OP.mult)
    ms(A("AC"), -0.484375)
    ts(r16, rf, 16.0, OP.mult)
    ts(A("K32"), A("K32"), r16, OP.add, 1184.0, OP.mult)
    ms(A("HF"), 0.5)
    scan(A("UP"), A("HF"), A("ZR"), 2.0 ** 96, OP.mult, OP.add)
    tt(A("UQ"), A("UP"), A("DM"), OP.mult)
    scan(A("WL"), A("KP"), A("UQ"), 0.0, OP.mult, OP.max)
    ts(A("TH", 0, LN), A("DR"), rf, OP.not_equal, -2.0 ** 99, OP.mult)
    ts(A("TH", LN, 384), A("UQ"), -4.0, OP.mult)
    ts(A("TH", 384, 576), A("UQ"), 2.0 ** -15, OP.mult)
    fill(A("CT", 0, 12))
    for k, c in enumerate((2240 + 2048.0, 2240.0, 2048.0, GS + 2240.0, GS + 2048.0)):
        ts(A("DT", 12 * k, 12 * k + 12), lane, c, OP.add)
    ts(A("R16"), A("REPf", 0, 4), 16.0, OP.mult, 15.0, OP.add)
    ts(r12, rf, 12.0, OP.mult)
    ts(A("INV1"), A("u24"), r12, OP.add)
    cp(A("D384"), ind(A("NI"), A("DUP")))
    tr(A("T384"), A("D384"))
    cp(A("L"), ind(A("T384"), A("PERM")))
    cp(A("NU0"), A("L"))

    for k in range(8):
        c0, c1 = 256 * k, 256 * k + 256
        b = (("pa", "pb"), ("ph", "px"), ("py", "pu"))[k % 3]
        sel, dif, wm = A("ga", c0, c1), A("gb", c0, c1), A("ma", c0, c1)
        ts(A("W", NM + c0, NM + c1), A("P2", c0, c1), 1.0 / 16, OP.mult, RND, OP.add)
        if PAR["qw"][k // 2] == "V":
            ts(A("W", c0, c1), A("P1", c0, c1), 1.0 / 16, OP.mult, RND, OP.add)
        else:
            act(A("W", c0, c1), A("P1", c0, c1), bias=RND, scale=1.0 / 16)
        lin(A(b[0], 256, 512), [("I1", A("P1", c0, c1)), ("Im1", A("P2", c0, c1))])
        lin(A(b[0], 0, 256), [("I1", A("W", c0, c1))])
        tt(sel, A(b[0], 0, 256), A("W", NM + c0, NM + c1), OP.is_le)
        tt(dif, A(b[0], 256, 512), sel, OP.mult)
        mm(A(b[1], 0, 256), A("I1"), A("P2", c0, c1), True, False)
        mm(A(b[1], 0, 256), A("I1"), dif, False, True)
        act(wm, A(b[1], 0, 256), bias=RND, scale=1.0 / 16)
        lin(A(b[0], 0, 256), [("I1", A("P2", c0, c1)), ("I1", dif), ("Im16", wm)])
        act(A("Y", c0, c1), A(b[0], 0, 256), bias=2064.0)

    def over(q, o, t, c0, c1):
        if q == "V":
            ts(o, A("W", c0, c1), 129.0 + LIMS[t], OP.is_ge, 1024.0, OP.mult)
        else:
            act(o, A("W", c0, c1), AF.Relu, bias=-1024.0 * (128 + LIMS[t]), scale=1024.0)

    def table(t, qs):
        for h in (0, 1):
            for k in range(4):
                over(qs[4 * h + k], A("G%d" % t, GS * h + 512 * k, GS * h + 512 * k + 512), t, NM * h + 512 * k, NM * h + 512 * k + 512)
            dadd(A("G%d" % t, GS * h, GS * h + NM), A("W", NM * h, NM * h + NM))
            behind("add")
            before("add")

    def table0():
        nd = PAR["nd"]
        for k in range(nd):
            c0, o0 = 512 * k, GS * (k // 4) + 512 * (k % 4)
            over(PAR["q0"][k], A("G0", o0, o0 + 512), 0, c0, c0 + 512)
            if k % 2:
                dadd(A("G0", o0 - 512, o0 + 512), A("W", c0 - 512, c0 + 512))
                before("add")
        for k in range(nd, 8):
            c0, c1 = 512 * k, 512 * k + 512
            b = A(("ph", "px", "py")[k % 3])
            over(PAR["q0"][k], A("J0", c0, c1), 0, c0, c1)
            lin(b, [("I1", A("W", c0, c1)), ("I1", A("J0", c0, c1))])
            o = A("G0", GS * (k // 4) + c0 % NM, GS * (k // 4) + c0 % NM + 512)
            if k in PAR.get("v0", ()):
                cp(o, b)
            else:
                act(o, b, AF.Copy)

    SPLIT = ((0, 72), (72, 144), (144, 192))

    def least(banks, out, spare):
        act(A("TR", 0, 72), A(banks[0], 12, 84) if spare else A(banks[0], 0, 72), AF.Copy)
        tt(A("TS"), A(banks[1], 0, 72), A("TR", 0, 72), OP.min)
        tt(A("TS", 0, 24), A("TS", 0, 24), A("TS", 48, 72), OP.min)
        if spare:
            tt(A("TS", 24, 36), A("TS", 24, 36), A("TR", 96, 108), OP.min)
        tt(A("TU", 0, 48), A(banks[2], 0, 48), A("TS", 0, 48), OP.min)
        tt(A("TU", 48, 72), A("TU", 0, 24), A("TU", 24, 48), OP.min)
        tt(out, A("TU", 48, 60), A("TU", 60, 72), OP.min)

    def rows(banks, j, bmat, src, stop=False):
        c0, c1 = SPLIT[j]
        for i in range(16):
            if banks[1] == "pz" and j == 0:
                lead = 12 if src == "ma" else 0
                o, r = A("pk", 12 - lead, 84), A(src, i - 16 * lead, 16 * c1, 16)
            else:
                o, r = A(banks[j], 0, c1 - c0), A(src, 16 * c0 + i, 16 * c1, 16)
            mm(o, A(bmat, 15 - i, 143 - i), r, False, stop and i == 15)

    def chunks(sizes):
        k = 0
        for s in sizes:
            yield k, k + s
            k += s

    def codes(tn, out):
        act(A("JJ"), A("XC"), AF.Relu, bias=-1024.0 * (128 + LIMS[tn]), scale=1024.0)
        lin(A("py", 0, 384), [("I1", A("XC")), ("I1", A("JJ"))])
        act(A(out), A("py", 0, 384), AF.Copy)

    def pairs(b, own, half, slot, stop=False):
        e = A("E", LN * slot + 16 * b, LN * slot + LN)
        ts(e, A("L16", LN * half + 16 * b, LN * half + LN), A("nar", own + b, own + b + 1), OP.is_equal,
           A("WL", 16 * b + 15, 16 * b + 16), OP.mult)
        mm(A("ph", 16 * b, LN), A("BO"), e, False, stop)

    def scatter(win, ou, o0, o1, src, piece):
        for c in range(0, o1 - o0, piece):
            cp(ind(A(win), A(ou, o0 + c, o0 + c + piece)), A(src, 16 * c, 16 * (c + piece)))

    wc, cc, f192, selr, f5, nb, c2, ty, c1y = [A("nar", 12 * k, 12 * k + 12) for k in range(9)]
    K2, K4 = ("pk", "pa", "pb"), ("pk", "pz", "pu")
    WU, CEU, SEL = A("WU"), A("CEU"), A("SEL")

    for t in range(3):
        NU, ZY, Gt, OU = "NU%d" % t, "ZY%d" % t, "G%d" % t, "OU%d" % (t % 2)
        z, yw = A(ZY, 0, LN), A(ZY, LN, 384)
        if t > 0:
            ops.append({"q": "G", "f": None, "w": [A(NU), z], "r": [], "kind": "arr", "t": t, "cost": 0.0, "lat": 0.0})
            cp(A("L"), A(NU))
        for h in (0, 1):
            mm(A("pz", LN * h, LN * h + LN), A("I1"), z, True, True)
        for j, (c0, c1) in enumerate(SPLIT):
            mm(A(K2[j], 0, c1 - c0), A("IF"), A("L", c0, c1), True, False)
        if t == 0:
            table0()
        fixed(True)
        for k0, k1 in chunks(PAR["ca"]):
            act(A("ga", 384 * k0, 384 * k1), ind(A("Y", 0, NM), A(NU, 24 * k0, 24 * k1)), AF.Copy)
        for k in range(8):
            tt(A("ma", 384 * k, 384 * k + 384), A("ga", 384 * k, 384 * k + 384), A("pz", 0, 384), OP.max)
            if k == 6:
                behind("s2")
        for j in range(3):
            rows(K2, j, "Bp2", "ga")
            rows(K2, j, "Bm4", "ma", True)
        least(K2, A("K0"), False)
        ts(A("WI"), A("K0"), 2047, OP.bitwise_and)
        cp(WU, A("WI"))
        act(yw, ind(A("Y", 0, NM), WU), AF.Copy)
        mm(A("pu", 0, LN), A("I1"), A("DG"), True, False)
        mm(A("pu", 0, LN), A("BOh"), yw, False, False)
        mm(A("pu", 0, LN), A("BOl"), yw, False, True)
        act(A("GW", 0, LN), ind(A(Gt, 0, NM), WU), AF.Copy)
        act(A("GW", LN, 384), ind(A(Gt, GS, GS + NM), WU), AF.Copy)
        for h in (0, 1):
            mm(A("pa", LN * h, LN * h + LN), A("I1"), A("GW", 0, LN), True, True)
            mm(A("pb", LN * h, LN * h + LN), A("I1"), A("GW", LN, 384), True, True)
        scan(A("ZS"), A("KP"), A("pu", 0, LN), 0.0, OP.mult, OP.max)
        cp(A("U0"), A("ZS", 15, LN, 16))
        ts(A("UI", 0, 12), A("U0"), 2047, OP.bitwise_and)
        tt(A("USQ"), A("UI", 0, 12), A("UI", 0, 12), OP.mult)
        ts(A("BS", 0, 12), A("USQ"), 1.0 / 32, OP.mult, A("AC"), OP.add)
        for c0, c1 in PAR["cc"]:
            rep = A("REP", c0 // 16, c1 // 16)
            tt(A("KU", c0, c1), ind(A("UI", 0, 12), rep), A("KT", c0, c1), OP.mult)
            tt(A("C0", c0, c1), ind(A("BS", 0, 12), rep), A("KU", c0, c1), OP.add)
            ts(A("CI", c0, c1), A("C0", c0, c1), 2047, OP.bitwise_and)
            cp(A("CU", c0, c1), A("CI", c0, c1))
        fixed(False)
        lin(A("px", 0, LN), [("I1", z), ("Im1", yw)])
        act(A("SZ%d" % t), A("px", 0, LN), AF.Abs)
        ts(wc, A("WI"), -1024.0, OP.add)
        ts(A("V0"), A("U0"), 1023, OP.bitwise_and)
        ts(A("VF", 0, 12), A("V0"), 2.0, OP.mult, 33.0, OP.add)
        tt(A("S7"), ind(A("VF", 0, 12), A("REP")), A("L"), OP.mult)
        tt(A("S8"), A("S7"), A("K32"), OP.add)
        ts(A("S9"), A("S8"), 5, OP.arith_shift_right, 2047, OP.bitwise_and)
        if t < 2:
            cp(A("SN%d" % t), A("S9"))
            add("G", (lambda v: lambda: send(v))(t + 1), None, [A("SN%d" % t), A("SZ%d" % t)], kind="send", t=t + 1, cost=500.0)
        else:
            cp(A("D384"), ind(A("S9"), A("INV1")))
            tr(A("T384"), A("D384"))
            cp(A("S7"), ind(A("T384"), A("INV2")))
            before("s4")
            store("Y", T.yn[:, :], A("S7"))
            store("Y", T.yz[:, :], A("SZ2"))
        tt(A("M17"), A("pa", 0, LN), A("GW", LN, 384), OP.min)
        ts(A("CT", 12, 204), A("CI"), -4095.0 * 4096, OP.add)
        for j, (c0, c1) in enumerate(((0, 84), (84, 156), (156, 204))):
            mm(A(K4[j], 0, c1 - c0), A("IF"), A("CT", c0, c1), True, False)
        na = PAR["na"]
        fixed(True)
        pages = (("ga", "ma", "pa", A(Gt, GS, GS + NM), A("GW", 0, LN)), ("gb", "mb", "pb", A(Gt, 0, NM), A("GW", LN, 384)))
        for h, m in na:
            got, low, own, win, gw = pages[h]
            tt(A(low, LN * m, LN * m + LN), ind(win, A("CU", 12 * m, 12 * m + 12)), gw, OP.min)
        for h, k0, k1 in PAR["cb"]:
            got, low, own, win, gw = pages[h]
            act(A(got, 384 * k0, 384 * k1), ind(win, A("CU", 24 * k0, 24 * k1)), AF.Copy)
            for k in range(k0, k1):
                tt(A(low, 384 * k, 384 * k + 384), A(got, 384 * k, 384 * k + 384), A(own, 0, 384), OP.min)
        behind("s4")
        for j in range(3):
            rows(K4, j, "Bp4", "ma")
            rows(K4, j, "Bp4", "mb", True)
        fixed(False)
        ts(f5, A("pk", 0, 12), 2600.0 * 4096, OP.is_ge, BIG, OP.mult)
        ts(f192, f5, 192.0, OP.min)
        tt(A("TR", 96, 108), f5, A("DT", 24, 36), OP.add)
        tt(ty, f5, A("WI"), OP.add)
        tt(selr, f192, lane, OP.add)
        cp(SEL, selr)
        fixed(True)
        least(K4, A("E0"), True)
        ts(A("CE"), A("E0"), 4095, OP.bitwise_and)
        fixed(False)
        if t == 0:
            table(1, PAR.get("q1", "VVVVVVVV"))
            table(2, PAR.get("q2", "SSSSSSSS"))
        for k in range(3):
            mm(A("ph", 0, LN), A("I1"), A("TH", LN * k, LN * k + LN), k == 0, False)
        fixed(False)
        cp(A("L16", 0, LN), ind(A("LC"), WU))
        for b in range(12):
            pairs(b, 0, 0, b)
        fixed(True)
        cp(CEU, A("CE"))
        ts(cc, A("CE"), -1024.0, OP.add)
        cp(A("L16", LN, 384), ind(A("LC"), CEU))
        for b in range(12):
            pairs(b, 12, 0, 12 + b)
            pairs(b, 0, 1, 24 + b)
            pairs(b, 12, 1, 36 + b, stop=(b == 11))
        fixed(False)
        act(A("PW", 0, LN), ind(A("P2", 0, NM), WU), AF.Copy)
        act(A("PW", LN, 384), ind(A("P1", 0, NM), WU), AF.Copy)
        act(A("WX", LN, 576), A("PW"), bias=RND, scale=1.0 / 16)
        for h in (0, 1):
            lin(A("px", LN * h, LN * h + LN),
                [("I1", A("PW", LN * h, LN * h + LN)), ("Im1", z), ("Im16", A("WX", LN * h + LN, LN * h + 384))])
        act(A("SG"), A("px", 0, 384), AF.Sign, bias=2064.0)
        act(A("NE"), A("SG"), AF.Abs)
        lin(A("py", 0, 384), [("I1", A("WX", LN, 576)), ("I1", A("NE"))])
        act(A("RR"), A("py", 0, 384), AF.Relu, bias=144.0, scale=-1.0)
        act(A("VV"), ind(A(ZY), SEL), AF.Copy)
        lin(A("px", 0, LN), [("Im16", A("RR", 0, LN)), ("I1", z)])
        lin(A("px", LN, 384), [("Im16", A("RR", LN, 384)), ("I1", z)])
        lin(A("py", 0, LN), [("I16", A("WX", 384, 576)), ("I1", yw)])
        act(A("P2", NM, NM + LN), A("px", 0, LN), bias=240.0)
        act(A("SP", 0, LN), A("px", LN, 384), bias=240.0)
        act(A("SP", LN, 384), A("py", 0, LN), bias=-2064.0)
        act(A("VP1", 0, LN), ind(A("SP"), SEL), AF.Copy)
        if t < 2:
            act(A("WX", 0, LN), A("RR", LN, 384), bias=144.0, scale=-1.0)
            act(A("XC", LN, 384), ind(A("WX", 0, 384), SEL), AF.Copy)
        act(A("XC", 0, LN), ind(A("P2", 0, 2240), CEU), bias=RND, scale=1.0 / 16)
        if t < 2:
            codes(t + 1, "VG")
        act(A("Y", NM, 2240), z, AF.Copy)
        act(A("YC"), ind(A("Y", 0, 2240), CEU), AF.Copy)
        act(A("WC"), ind(A("P1", 0, 2240), CEU), bias=RND, scale=1.0 / 16)
        lin(A("px", 0, LN), [("I16", A("XC", 0, LN)), ("I1", A("VV"))])
        lin(A("px", LN, 384), [("I16", A("WX", LN, 384)), ("I1", A("YC"))])
        act(A("VP2"), A("px", 0, 384), bias=-2064.0)
        lin(A("py", 0, LN), [("I16", A("WC")), ("I1", A("YC"))])
        act(A("VP1", LN, 384), A("py", 0, LN), bias=-2064.0)
        if t == 0:
            codes(2, "VD")
        ts(nb, A("E0"), 450.0 * 4096, OP.is_ge, BIG, OP.mult)
        cp(A("TT", 24, 36), A("CE"))
        tt(A("TT", 12, 24), nb, A("WI"), OP.add)
        ts(c1y, A("CE"), 2240.0, OP.add)
        tt(A("TT", 0, 12), c1y, ty, OP.min)
        if t < 2:
            ts(c2, A("CE"), float(GS), OP.add)
            ts(A("TT", 36, 48), A("TT", 12, 24), float(GS), OP.add)
            tt(A("TT", 48, 60), c2, ty, OP.min)
        fixed(True)
        scan(A("ZS"), A("KP"), A("ph", 0, LN), 0.0, OP.mult, OP.max)
        ts(A("OA"), ind(A("ZS"), A("R16")), 0.0, OP.is_gt, BIG, OP.mult)
        tt(A("OB"), A("OA"), A("TT"), OP.add)
        tt(A("OF"), A("OB"), A("DT"), OP.min)
        cp(A(OU), A("OF"))
        if t < 2:
            cp(ind(A("Y"), A(OU, 0, 12)), A("VP1", LN, 384))
            fixed(False)
            fill(A("P1", NM, 2240))
            scatter("G%d" % (t + 1), OU, 36, 60, "VG", PAR["piece"])
            before("s2")
            add("S", lambda: S.activation(ap(A("EX", 0, 12)), ap(A("OF", 24, 36)), AF.Sign, bias=-2047.5, scale=1.0,
                                          accum_out=ap(A("EX", 12, 13))), A("EX", 0, 13), [A("OF", 24, 36)])
            mm(A("pu", 0, 1), A("ONE"), A("EX", 12, 13), True, True)
            act(A("AC"), A("pu", 0, 1), bias=768.0 - 0.484375, scale=-0.5)
            scatter("P2", OU, 12, 36, "VP2", PAR["piece"])
            scatter("P1", OU, 12, 24, "VP1", PAR["piece"])
            if t == 0:
                scatter("G2", OU, 36, 60, "VD", PAR["piece"])
                before("s4")
        else:
            scatter("P2", OU, 12, 36, "VP2", 24)
            store("Y", T.ys[:, 0:1024], A("P2", 0, 1024))
            store("S", T.ys[:, 1024:NM], A("P2", 1024, NM))
            ts(A("OU1", 0, 12), A("OF", 12, 24), 2240.0, OP.add)
            cp(A("OU1", 12, 24), A("OF", 0, 12))
            cp(ind(A("Y"), A("OU1", 0, 24)), A("VP1"))
            for k in range(32):
                mm(A("px", 0, 64), A("I1"), A("P1", 64 * k, 64 * k + 64), k == 0, k == 31)
            cp(A("YF"), A("px", 0, 64))
            store("Y", T.yf[:, :], A("YF"))
